import numpy as np, ml_dtypes
CORES = [6,15,38,47]
N = 4
BF = ml_dtypes.bfloat16
def gentries(a):
    return np.ascontiguousarray(a.reshape(8, 16, -1).transpose(0, 2, 1)).reshape(8, -1)
def gtable(e):
    e = np.asarray(e); return np.ascontiguousarray(e.reshape(8, -1, 16).transpose(0, 2, 1)).reshape(128, -1).astype(np.int32)
V, W, U, ND, G, K, B, H = 768, 1024, 4, 2, 128, 4, 2, 2
KV, Q, TOPS, TH, FA, FB = K * V, 8, 2 ** 20 - 1, 7340025, 0.1875, 0.3125
def pick(t, c):
    return np.take_along_axis(t, c[:, None, :], 2)
def lend(t, sl):
    res = []
    for r in range(N):
        w = [t[r]]
        for e in range(ND):
            q = (r + e + 1) % N; w.append(pick(t[q], sl[q, :, e]))
        res.append(np.concatenate(w, axis=2))
    return np.stack(res)
def home(a, sl, both):
    res = []
    for q in range(N):
        o = a[q][:, :, :V]
        for e in range(ND):
            r = (q - e - 1) % N; b = np.zeros((8, 16, V), a.dtype)
            np.put_along_axis(b, sl[q, :, e][:, None, :], a[r][:, :, V + e * G:V + (e + 1) * G], 2)
            o = both(o, b)
        res.append(o)
    return np.stack(res)
def drop(z, x, both):
    b = np.zeros((8, 16, U * W), x.dtype)
    np.put_along_axis(b, z[:, None, :], x, 2)
    return both.reduce(b.reshape(8, 16, U, W), axis=2)
def coarse(cl, cr, snd, cu):
    c = cu & (W - 1); rule = np.repeat(cr, V, axis=4)
    t = lend(cl, snd[:, :, 0])
    s1 = np.stack([pick(t[r], c[r, :, 0, 0]) + pick(t[r], c[r, :, 0, 1]) + rule[r, :, :, 0] for r in range(N)])
    t = lend(np.maximum.reduce(s1.reshape(N, 8, 16, K, V), axis=3), snd[:, :, 1])
    s2, a = [], []
    for r in range(N):
        x, y = pick(t[r], c[r, :, 1, 0]), pick(t[r], c[r, :, 1, 1]); w = rule[r, :, :, 1]
        s2.append(x + y + w)
        a.append(np.maximum(drop(cu[r, :, 1, 0], y + w, np.maximum), drop(cu[r, :, 1, 1], x + w, np.maximum)))
    o = home(np.stack(a), snd[:, :, 1], np.maximum)
    return s1 + np.tile(o, (1, 1, 1, K)), np.stack(s2)
def parts(rng):
    d = {}
    d["cl"] = rng.integers(0, 2 ** 19, (N, 8, 1, V)) + rng.integers(0, 2 ** 19, (N, 8, 16, V))
    d["cr"] = rng.integers(0, 2 ** 19, (N, 8, 16, 2, K))
    d["cu"] = np.ascontiguousarray(np.argsort(rng.random((N, 8, 2, 2, U * W)), axis=-1)[..., :KV])
    d["fu"] = np.ascontiguousarray(np.argsort(rng.random((N, 8, 2, H, 2, U * W)), axis=-1)[..., :KV])
    d["snd"] = np.ascontiguousarray(np.argsort(rng.random((N, 8, 2, ND, V)), axis=-1)[..., :G])
    d["fl"] = 0.8 + 0.4 * rng.random((N, 8, 16, V))
    d["fw"] = FA + (FB - FA) * rng.random((N, 8, 16, 2, B * H))
    d["top"] = 0.5 + 1.5 * rng.random((N, 8, 16, V))
    return d
def bound(rng, p, lo, hi):
    s = np.sort(p[..., ::16], axis=-1); x = lo + (hi - lo) * rng.random((N, 8, 1, 1)) + 0.04 * rng.random((N, 8, 16, 1))
    return np.take_along_axis(s, (x * s.shape[-1]).astype(np.int64), 3)[..., 0]
def finish(rng, d, lo, hi):
    p = coarse(d["cl"], d["cr"], d["snd"], d["cu"])
    d["th"] = np.stack([bound(rng, p[0], lo, hi), bound(rng, p[1], lo, hi)], axis=-1)
    return d
def pack(d):
    e = {}
    for k in ("cl", "cr", "th"): e[k] = np.ascontiguousarray(d[k].reshape(N, 128, -1)).astype(np.int32)
    for k in ("cu", "fu", "snd"): e[k] = np.stack([gtable(a.reshape(8, -1)) for a in d[k]])
    e["fl"] = d["fl"].reshape(N, 128, V).astype(np.float32).astype(BF)
    e["fw"] = np.clip(d["fw"].reshape(N, 128, 2 * B * H), FA, FB).astype(np.float32)
    e["top"] = d["top"].reshape(N, 128, V).astype(np.float32).astype(BF)
    return e
def setup_inputs(rng):
    return pack(finish(rng, parts(rng), 0.4, 0.56))
def setup_inputs_brink(rng):
    d = parts(rng)
    d["cl"] = rng.integers(2 ** 19, 2 ** 20 - 8, (1, 8, 16, 1)) + rng.integers(0, 4, (N, 8, 16, V))
    d["cr"] = rng.integers(2 ** 19, 2 ** 20 - 8, (1, 8, 16, 1, 1)) + rng.integers(0, 2, (N, 8, 16, 2, K))
    return pack(finish(rng, d, 0.45, 0.56))
def crowd(rng, n):
    x = np.array([0, W - 1, V - 1, V]); o = np.concatenate([x, rng.permutation(np.setdiff1d(np.arange(W), x))])
    z = (o[:, None] + W * np.arange(U)[None, :]).reshape(-1)[:KV + KV // 8]
    return np.stack([rng.permutation(z)[:KV] for i in range(n)])
def setup_inputs_calm(rng):
    d = parts(rng); o = rng.permutation(8); full = o[0]; unit = 2.0 ** -10
    d["snd"] = np.ascontiguousarray(np.argsort(rng.random((N, 8, 2, V)), axis=-1)[..., :ND * G].reshape(N, 8, 2, ND, G))
    d["top"] = unit * (8 + 4 * rng.random((N, 8, 16, V)))
    d["top"][:, full] = unit * np.maximum(1.0, 0.75 + 0.5 * rng.random((N, 16, V)))
    kinds = ((0.25, 0.25, 0, 1), (0.25, 0.25, 1, 1), (0.05, 0.25, 1, 2), (0.02, 0.1, 1, 1))
    for i, (a, b, t1, t2) in enumerate(kinds):
        g = o[i + 1]
        d["cl"][:, g] = rng.random((N, 16, V)) < a
        d["cr"][:, g] = rng.random((N, 16, 2, K)) < b
        if i < 2:
            d["top"][:, g] = 0.5 * d["top"][:, g]
            for q in range(N):
                z = crowd(rng, 1)[0]; d["cu"][q, g, 1, 0] = z; d["cu"][q, g, 1, 1] = rng.permutation(z)
    d["snd"][:, full, :, :, 1:G - 1] = 1 + np.argsort(rng.random((N, 2, ND, V - 2)), axis=-1)[..., :G - 2]
    d["snd"][:, full, :, :, 0] = V - 1; d["snd"][:, full, :, :, G - 1] = 0
    e = V + G * np.arange(ND); most = np.concatenate([np.array([V - 1, 0]), e, e + G - 1])
    must = (most[:, None] + W * np.arange(U)[None, :]).reshape(-1); lack = W * (U - 1); rest = np.setdiff1d(np.arange(U * W), must)
    for q in range(N):
        for m in range(2):
            for h in range(H):
                for s in range(2):
                    first, last = must, must[:0]
                    if h == H - 1 and s == 1: first, last = must[must != lack], must[must == lack]
                    z = rng.permutation(rest); n = B * V - len(first); k = KV - B * V - len(last)
                    d["fu"][q, full, m, h, s] = np.concatenate([rng.permutation(np.concatenate([first, z[:n]])), rng.permutation(np.concatenate([last, z[n:n + k]]))])
    d = finish(rng, d, 0.4, 0.56); d["th"][:, full] = 0
    for i, (a, b, t1, t2) in enumerate(kinds):
        g = o[i + 1]
        for q in range(N):
            for m, t in enumerate((t1, t2)):
                d["th"][q, g, :, m] = t + 1; d["th"][q, g, rng.permutation(16)[:7], m] = t
    return pack(d)
def unused_felt(d, q, g):
    def uses(r):
        u = np.zeros(W, bool); u[d["cu"][r, g, 1] & (W - 1)] = True
        return u
    used = uses(q)[:V]
    for e in range(ND):
        s = d["snd"][q, g, 1, e]; used[s] = used[s] | uses((q - e - 1) % N)[V + e * G:V + (e + 1) * G]
    named = np.zeros(W, bool); named[d["fu"][q, g, 1][:, :, :B * V] & (W - 1)] = True
    return bool(np.any(named[:V] & ~used))
def setup_inputs_corners(rng):
    d = parts(rng); o = rng.permutation(8); few, full, rest = o[:2], o[2:4], o[4:]; lone = o[4]
    rest = rest[1:]
    d["snd"] = np.ascontiguousarray(np.argsort(rng.random((N, 8, 2, V)), axis=-1)[..., :ND * G].reshape(N, 8, 2, ND, G))
    d["top"] = 0.75 + 0.5 * rng.random((N, 8, 16, V)); d["top"][:, full] = d["top"][:, full] * 0.375
    for q in range(N):
        for g in few:
            d["cl"][q, g] = rng.integers(0, 1024, (16, V))
            for m in range(2):
                a = np.zeros(K, bool); i = int(rng.integers(0, 4))
                if i == 0: a[0] = True
                elif i == 1: a[K - 1] = True
                elif i == 2: a[:] = True
                else: a[1:] = True
                d["cr"][q, g, :, m] = np.where(a, TOPS, 0)
        for g in full:
            d["cu"][q, g] = crowd(rng, 4).reshape(2, 2, KV); d["fu"][q, g] = crowd(rng, 4 * H).reshape(2, H, 2, KV)
        g = full[0]; d["cu"][q, g, :, 1] = d["cu"][q, g, :, 0]; d["fu"][q, g, :, :, 1] = d["fu"][q, g, :, :, 0]
        d["cu"][q, lone, 1] = crowd(rng, 2)
    d = finish(rng, d, 0.4, 0.56); d["th"][:, few] = 5 * 2 ** 19
    for q in range(N):
        many, dead = 15 + q % 2, (Q - 1) * (1 - (q // 2) % 2)
        cases = ((many, many), (Q, Q), (Q, dead) if q % 2 == 0 else (dead, 16))
        for i, g in enumerate([lone] + list(rng.permutation(rest)[:2])):
            for m, n in enumerate(cases[i]):
                d["th"][q, g, :, m] = TH; d["th"][q, g, rng.permutation(16)[:n], m] = 0
    assert any(unused_felt(d, q, lone) for q in range(N))
    return pack(d)
def setup_inputs_ends(rng):
    d = parts(rng)
    col = rng.random((N, 8, 1, V)) < 0.85; flip = rng.random((N, 8, 16, V)) < 0.05
    d["cl"] = np.where(col ^ flip, TOPS, 0); d["cl"][..., V - 1] = TOPS; d["cl"][..., V - 2] = 0
    d["cr"] = np.where(rng.random((N, 8, 16, 2, K)) < 0.6, TOPS, 0); d["cr"][:, :, 15, :, K - 1] = TOPS
    th = np.full((N, 8, 16, 2), TH, np.int64)
    for g in range(8):
        i = rng.permutation(15); d["cl"][:, g, i[0]] = 0; d["cr"][:, g, i[0]] = 0
        for q in range(N):
            for m in range(2):
                n = 7 if g == 7 or q == N - 1 else int(rng.choice(np.array([6, 7, 7, 8])))
                th[q, g, i[:n], m] = 0
    d["th"] = th
    d["cr"][N - 1, 7, :, 1, 0] = np.minimum(d["cr"][N - 1, 7, :, 1, 0], TOPS - 1); d["cr"][N - 1, 7, 15, 1, 0] = TOPS - 1
    e = np.concatenate([np.arange(G // 2), np.arange(V - G // 2, V)]); d["snd"] = e[np.argsort(rng.random((N, 8, 2, ND, G)), axis=-1)]
    e = np.concatenate([np.arange(KV // 2), np.arange(U * W - KV // 2, U * W)])
    d["cu"] = e[np.argsort(rng.random((N, 8, 2, 2, KV)), axis=-1)]; d["fu"] = e[np.argsort(rng.random((N, 8, 2, H, 2, KV)), axis=-1)]
    d["fl"] = np.where(rng.random((N, 8, 16, V)) < 0.5, 0.75, 1.25)
    d["fw"] = np.where(rng.random((N, 8, 16, 2, B * H)) < 0.5, FA, FB)
    d["top"] = np.where(rng.random((N, 8, 16, V)) < 0.9, 32.0, 2.0 ** -10)
    return pack(d)
def setup_inputs_spread(rng):
    d = parts(rng)
    d["cl"] = np.minimum((np.exp2(20 * rng.random((N, 8, 1, V))) * (0.25 + 0.75 * rng.random((N, 8, 16, V)))).astype(np.int64), TOPS)
    d["cr"] = np.minimum(np.exp2(20 * rng.random((N, 8, 16, 2, K))).astype(np.int64), TOPS)
    d["fl"] = np.clip(0.75 + 0.5 * rng.random((N, 8, 1, V)) + 0.1 * (rng.random((N, 8, 16, V)) - 0.5), 0.75, 1.25)
    d["top"] = np.exp2(2 * rng.random((N, 8, 1, V)) - 1) * (0.75 + 0.5 * rng.random((N, 8, 16, V)))
    return pack(finish(rng, d, 0.4, 0.56))
def unlist(a, shape):
    return np.stack([gentries(x) for x in a]).astype(np.int64).reshape((N, 8) + shape)
def check_ranges(d):
    bad = []
    for k, lo, hi in (("cl", 0, TOPS), ("cr", 0, TOPS), ("th", 0, TH), ("cu", 0, U * W - 1), ("fu", 0, U * W - 1), ("snd", 0, V - 1)):
        if np.min(d[k]) < lo or np.max(d[k]) > hi: bad.append("range of " + k)
    for k, lo, hi in (("fl", 0.75, 1.25), ("fw", FA, FB), ("top", 2.0 ** -10, 32.0)):
        x = np.asarray(d[k]).astype(np.float64)
        if not np.all((x >= lo) & (x <= hi)): bad.append("range of " + k)
    for k, n in (("cu", KV), ("fu", KV), ("snd", G)):
        s = np.sort(unlist(d[k], (-1, n)), axis=-1)
        if np.any(s[..., 1:] == s[..., :-1]): bad.append("repeated numbers in a block of " + k)
    return bad
def reference(cl, cr, th, cu, fu, snd, fl, fw, top):
    sl = unlist(snd, (2, ND, G)); cz = unlist(cu, (2, 2, KV)); fz = unlist(fu, (2, H, 2, KV)); fc = fz & (W - 1)
    p = coarse(cl.astype(np.int64).reshape(N, 8, 16, V), cr.astype(np.int64).reshape(N, 8, 16, 2, K), sl, cz)
    t = th.astype(np.int64).reshape(N, 8, 16, 2)
    counted, place = [], []
    for m in range(2):
        votes = np.add.reduce((p[m] >= t[:, :, :, m:m + 1]).astype(np.int64), axis=2)
        live = (votes >= Q).astype(np.int64).reshape(N, 8, K, V)
        before = np.add.accumulate(live, axis=2) - live
        counted.append(((live == 1) & (before < B)).reshape(N, 8, KV)); place.append(np.minimum(before, B - 1).reshape(N, 8, KV))
    wts = fw.astype(np.float64).reshape(N, 8, 16, 2, B * H)
    def weight(r, m, h):
        return pick(wts[r, :, :, m], place[m][r] * H + h) * counted[m][r][:, None, :]
    x = fl.astype(np.float64).reshape(N, 8, 16, V); known = []
    for m in range(2):
        known.append(lend(x, sl[:, :, m])); res = []
        for r in range(N):
            y = np.zeros((8, 16, V))
            for h in range(H):
                e = pick(known[m][r], fc[r, :, m, h, 0]) * pick(known[m][r], fc[r, :, m, h, 1]) * weight(r, m, h)
                y = y + np.add.reduce(e.reshape(8, 16, K, V), axis=2)
            res.append(y)
        x = np.stack(res)
    o = top.astype(np.float64).reshape(N, 8, 16, V)
    for m in (1, 0):
        res = []
        for r in range(N):
            a = np.zeros((8, 16, W))
            for h in range(H):
                e = np.tile(o[r], (1, 1, K)) * weight(r, m, h)
                a = a + drop(fz[r, :, m, h, 0], e * pick(known[m][r], fc[r, :, m, h, 1]), np.add) + drop(fz[r, :, m, h, 1], e * pick(known[m][r], fc[r, :, m, h, 0]), np.add)
            res.append(a)
        o = home(np.stack(res), sl[:, :, m], np.add)
    return {"yi": x.reshape(N, 128, V).astype(np.float32), "yo": o.reshape(N, 128, V).astype(np.float32)}

def check_inputs(d):
    bad = list(check_ranges(d))
    if not bad:
        for name, y in reference(**d).items():
            for q in range(N):
                v = np.abs(np.asarray(y[q], np.float64)); s = np.sqrt(np.mean(v * v))
                if v.max() > 15 * s or s < 2.0 ** -10: bad.append('%s of rank %d is uneven or too small' % (name, q))
    return bad

@@ -1,0 +1,506 @@
+from concourse.bass import DstId, RemoteDMATransfer
+from concourse.mybir import AluOpType as A, ActivationFunctionType as F
+
+V, W, G, KV = 768, 1024, 128, 3072
+WW = 4992
+BIG = 2.0 ** 40
+SIDES = ((0, V // 2), (V // 2, V))
+f32, bf, i32, u16 = "float32", "bfloat16", "int32", "uint16"
+
+SCRATCH = {}
+for _n in range(6):
+    SCRATCH["W%d" % _n] = ("sbuf", [128, WW], f32)
+for _n, _c, _t in [
+    ("BA", KV, f32), ("BB", KV, f32), ("BC", KV + 64, f32), ("BD", KV, f32), ("BE", KV, f32),
+    ("VB", KV, bf), ("clw", W, f32), ("c1w", W, f32), ("flw", W + 16, bf), ("i1w", W + 16, f32),
+    ("A1", W, f32), ("A2", V, f32), ("A3", V, f32), ("sa", 256, f32), ("sb", 256, f32), ("sf", 256, bf),
+    ("ld", 768, f32), ("tm", 256, f32), ("cli", V, i32), ("cui", V, i32), ("fui", 2 * V, i32),
+    ("sndi", 32, i32), ("cri", 8, i32), ("thi", 8, i32), ("fwf", 8, f32), ("sm", 16, f32), ("topb", V, bf),
+    ("cc", V, u16), ("pl", 384, u16), ("inv", 512, u16), ("fc", V, u16), ("fz", V, u16), ("sndu", 32, u16),
+    ("CC", V, bf), ("DU", 192, f32), ("E", 144, bf), ("ID", 128, f32),
+]:
+    SCRATCH[_n] = ("sbuf", [128, _c], _t)
+for _n, _c in [("PA", 1024), ("PB", 1024), ("PC", 1024), ("PV0", 512), ("PV1", 512)]:
+    SCRATCH[_n] = ("psum", [128, _c], f32)
+
+NDMA = 40
+SEMAPHORES = ["v", "s", "p", "c"] + ["d%d" % _i for _i in range(NDMA)] + ["x%d" % _i for _i in range(7)] + ["l%d" % _i for _i in range(7)]
+PE_SUM = 0
+EARLY = "v"
+RW_S = (0,)
+PRE_H = 4
+PRE_I = 4
+NV = 3
+FOLD2 = True
+
+
+def rank_program(g, core, T, topo):
+    rank = T.rank_of(core)
+    if rank is None:
+        return
+    N = len(T.cores)
+    queue = {"v": g.vector, "s": g.scalar, "p": g.tensor, "g": g, "y": g.sync}
+    own = {"v": "v", "s": "s", "p": "p", "g": "c"}
+    count, waited, log, ndma = {}, {q: {} for q in queue}, {}, [0]
+
+    def R(name, a=0, b=None, step=1):
+        if b is None:
+            b = T[name].shape[1]
+        ap = T[name][:, a:b] if step == 1 else T[name][:, a:b:step]
+        return (ap, [(name, a, b)], [])
+
+    def IX(win, off):
+        return (win[0].indirect(off[0]), win[1], off[1])
+
+    def span(name, a, b):
+        if SCRATCH[name][0] == "psum":
+            return a // 512 * 512, -(-b // 512) * 512
+        return a, b
+
+    def wait(q, tickets):
+        need = {}
+        for sem, val in tickets:
+            need[sem] = max(need.get(sem, 0), val)
+        for sem, val in need.items():
+            if waited[q].get(sem, 0) < val:
+                queue[q].wait_ge(T.sem[sem], val)
+                waited[q][sem] = val
+
+    def deps(q, reads, writes, compute):
+        res = []
+        for regs, isw in ((reads, False), (writes, True)):
+            for name, a, b in regs:
+                ps = SCRATCH[name][0] == "psum"
+                for a2, b2, w2, q2, tk in log.get(name, []):
+                    mine = compute and q2 == q
+                    if ps and not mine:
+                        lo, hi = span(name, a, b)
+                        lo2, hi2 = span(name, a2, b2)
+                        if lo < hi2 and lo2 < hi:
+                            res.append(tk)
+                    elif a < b2 and a2 < b and (w2 or isw):
+                        if mine and isw and q == "p":
+                            continue
+                        res.append(tk)
+        return res
+
+    def note(q, reads, writes, tk):
+        for regs, isw in ((reads, False), (writes, True)):
+            for name, a, b in regs:
+                log.setdefault(name, []).append((a, b, isw, q, tk))
+
+    def op(q, outs, ins, emit, apart=False):
+        writes = [r for o in outs for r in o[1]]
+        reads = [r for o in outs for r in o[2]] + [r for x in ins for r in x[1] + x[2]]
+        wait(q, deps(q, reads, [] if apart else writes, True))
+        sem = own[q]
+        count[sem] = count.get(sem, 0) + 1
+        emit().then_inc(T.sem[sem], 1)
+        note(q, reads, writes, (sem, count[sem]))
+
+    def dma(q, pairs, after=(), **kw):
+        sem = "d%d" % ndma[0]
+        ndma[0] += 1
+        writes = [r for o, x in pairs for r in o[1]]
+        reads = [r for o, x in pairs for r in x[1]]
+        wait(q, deps(q, reads, writes, False) + list(after))
+        for o, x in pairs:
+            queue[q].dma_start(o[0], x[0], **kw).then_inc(T.sem[sem], 16)
+        count[sem] = 16 * len(pairs)
+        note("dma", reads, writes, (sem, count[sem]))
+
+    def H(name):
+        return (T[name][:], [], [])
+
+    def exchange(n, sign, src, dst):
+        name, a = src
+        name2, a2 = dst
+        reads = [(name, a, a + 2 * G)]
+        wait("g", deps("g", reads, [], False))
+        trs, total = [], 0
+        for d in (1, 2):
+            peer = T.cores[(rank + sign * d) % N]
+            eng = topo.engines(core, peer)
+            half = len(eng) // 2
+            mine = eng[:half] if d == 1 else eng[half:2 * half]
+            rid, pid, _se = topo.addr(peer)
+            trs.append(RemoteDMATransfer(dst_ids=[DstId(rid=rid, pnc=pid)], dma_engine_mask=sum(1 << e for e in mine),
+                                         remote_sem=T.sem["x%d" % n], src=T[name][:, a + (d - 1) * G:a + d * G],
+                                         dst=T[name2][:, a2 + (d - 1) * G:a2 + d * G]))
+            total += len(mine)
+        g.remote_dma_fused(trs, local_sem=T.sem["l%d" % n])
+        count["l%d" % n] = total
+        note("dma", reads, [], ("l%d" % n, total))
+        come = sum(len(topo.engines(T.cores[(rank - sign * d) % N], core)) // 2 for d in (1, 2))
+        count["x%d" % n] = come
+        note("dma", [], [(name2, a2, a2 + 2 * G)], ("x%d" % n, come))
+        return ("x%d" % n, come)
+
+    def val(x):
+        return x[0] if isinstance(x, tuple) else x
+
+    def aps(*xs):
+        return [x for x in xs if isinstance(x, tuple)]
+
+    def cp(o, x):
+        op("v", [o], [x], lambda: g.vector.tensor_copy(o[0], x[0]))
+
+    def tt(o, x, y, f, apart=False):
+        op("v", [o], [x, y], lambda: g.vector.tensor_tensor(o[0], x[0], y[0], f), apart)
+
+    def ts(o, x, s1, f1, s2=None, f2=None):
+        if f2 is None:
+            op("v", [o], aps(x, s1), lambda: g.vector.tensor_scalar(o[0], x[0], val(s1), None, f1))
+        else:
+            op("v", [o], aps(x, s1, s2), lambda: g.vector.tensor_scalar(o[0], x[0], val(s1), val(s2), f1, f2))
+
+    def scan(o, x, y):
+        op("v", [o], [x, y], lambda: g.vector.tensor_tensor_scan(o[0], x[0], y[0], 0.0, A.mult, A.add))
+
+    def fill(o, c):
+        op("v", [o], [], lambda: g.vector.memset(o[0], c))
+
+    def act(o, x, f, **kw):
+        op("s", [o], aps(x, *kw.values()), lambda: g.scalar.activation(o[0], x[0], f, **{k: val(a) for k, a in kw.items()}))
+
+    def iota(o, pat, base, cm):
+        op("g", [o], [], lambda: g.iota(o[0], pat, base, cm, allow_small_or_imprecise_dtypes=True))
+
+    def keep(o, pat, cmp, other, base, cm):
+        op("g", [o], [o], lambda: g.affine_select(o[0], o[0], pat, cmp, other, base, cm))
+
+    def mm(o, terms, first=True, last=True):
+        def emit():
+            ins = None
+            for n, (l, r) in enumerate(terms):
+                ins = g.tensor.matmul(o[0], l[0], r[0], first and n == 0, last and n == len(terms) - 1)
+            return ins
+        op("p", [o], [x for t in terms for x in t], emit)
+
+    def piece(name, k, base=0):
+        return R(name, base + k * V, base + (k + 1) * V)
+
+    def lst(name, a, n=48):
+        return R(name, a, a + n)
+
+    def col(name, a):
+        return R(name, a, a + 1)
+
+    dma("y", [(R("sndi"), H("snd"))])
+    dma("s", [(R("cli"), H("cl"))])
+    dma("y", [(R("cui"), H("cu"))])
+    dma("g", [(R("topb"), H("top"))])
+    dma("y", [(R("cri"), H("cr")), (R("thi", 0, 2), H("th")), (R("fwf"), H("fw"))])
+    dma("y", [(R("flw", 0, V), H("fl")), (R("fui"), H("fu"))])
+    fill(R("W4", 0, W), 0.0)
+    fill(R("W4", W, 2 * W), 0.0)
+    fill(R("BC", 0, 64), 0.0)
+    fill(R("flw", W, W + 16), 0.0)
+    fill(R("i1w", W, W + 16), 0.0)
+    act(R("W4", 2 * W, 3 * W), R("W4", 0, W), F.Copy)
+    act(R("W4", 3 * W, 4 * W), R("W4", 0, W), F.Copy)
+    act(R("W3", 0, W), R("W4", 0, W), F.Copy)
+    iota(piece("BA", 0), [[1, V]], 64, 0)
+    cp(R("sndu"), R("sndi"))
+    cp(R("sa"), IX(R("cli"), lst("sndu", 0, 16)))
+    x0 = exchange(0, -1, ("sa", 0), ("clw", V))
+    for k in (1, 2, 3):
+        iota(piece("BA", k), [[1, V]], 64 + k * V, 0)
+    act(R("sf"), IX(R("flw", 0, V), lst("sndu", 0, 16)), F.Copy)
+    exchange(1, -1, ("sf", 0), ("flw", V))
+    cp(R("clw", 0, V), R("cli"))
+    ts(R("cli", 0, 384), R("cui", 384, V), 4, A.arith_shift_right)
+    ts(R("cli", 384, V), R("cui", 0, 384), W - 1, A.bitwise_and)
+    ts(R("A1", 0, 384), R("cli", 0, 384), -4095.0 / 256.0, A.mult)
+    cp(R("cc", 0, 384), R("cli", 384, V))
+    tt(R("A1", 384, V), R("cui", 384, V), R("A1", 0, 384), A.add)
+    ts(R("pl"), R("A1", 384, V), 256.0, A.mult)
+    cp(R("sm", 0, 8), R("cri"))
+    cp(R("sm", 8, 10), R("thi", 0, 2))
+    ts(col("sm", 10), col("thi", 1), -1.0, A.mult, 0.5, A.add)
+    dma("y", [(R("W5", u * W, (u + 1) * W), R("W3", 0, W)) for u in range(4)], after=[x0])
+    dma("y", [(R("W3", u * W, (u + 1) * W), R("W3", 0, W)) for u in range(1, 4)])
+
+    def invert(q, s, k):
+        o = IX(R("W%d" % (4 + s), 0, 4 * W), lst("pl", s * 192 + k * 48))
+        if q == "s":
+            act(o, piece("BA", k), F.Silu)
+        else:
+            cp(o, piece("BA", k))
+
+    def rewrap(s):
+        name = "W%d" % (4 + s)
+        dma("y", [(R("A2", s * 256, (s + 1) * 256), (T[name][0:128:18, 0:4 * W], [(name, 0, 4 * W)], []))])
+
+    if EARLY:
+        invert(EARLY, 0, 0)
+
+    def join(name, base, out, f, k0):
+        for k in range(k0, 4):
+            for a, b in SIDES:
+                tt(R(out if k == 3 else "PA", a, b), R("PA", a, b), R(name, base + k * V + a, base + k * V + b), f)
+
+    for k in range(4):
+        act(piece("BB", k), IX(R("clw"), lst("cc", k * 48)), F.Identity, bias=col("sm", k))
+    for k in range(4):
+        tt(piece("BB", k), IX(R("clw"), lst("cc", 192 + k * 48)), piece("BB", k), A.add)
+    act(R("PA", 0, V), piece("BB", 0), F.Copy)
+    join("BB", 0, "c1w", A.max, 1)
+    cp(R("sb"), IX(R("c1w", 0, V), lst("sndu", 16, 16)))
+    exchange(2, -1, ("sb", 0), ("c1w", V))
+    iota(R("E"), [[0, 144]], 1, 0)
+    iota(R("CC", 0, 384), [[0, 384]], 8, 0)
+    iota(R("CC", 384, V), [[0, 384]], 0, 0)
+    iota(R("ID"), [[0, 128]], 1, 0)
+    iota(R("DU"), [[0, 4], [16, 48]], 4 * W, 1)
+    keep(R("E"), [[1, 144]], A.is_ge, 0.0, 0, -1)
+    for n in range(4):
+        keep(R("CC", n * 192, (n + 1) * 192), [[0, 48], [1, 4]], A.is_gt, 1e9 if n % 2 else -1e9, 0, 0)
+    keep(R("E"), [[-1, 144]], A.is_ge, 0.0, 15, 1)
+    keep(R("ID"), [[-1, 128]], A.is_equal, 0.0, 0, 1)
+    keep(R("E"), [[0, 9], [1, 16]], A.is_ge, 0.0, -15, 0)
+    for k in range(1 if EARLY else 0, 4):
+        invert("s", 0, k)
+    rewrap(0)
+    ts(R("cli", 0, 384), R("cui", 384, V), W - 1, A.bitwise_and)
+    invert("v", 1, 0)
+    cp(R("cc", 384, V), R("cli", 0, 384))
+    invert("v", 1, 1)
+
+    for k in range(4):
+        act(piece("BC", k, 64), IX(R("c1w"), lst("cc", 384 + k * 48)), F.Identity, bias=col("sm", 4 + k))
+    for k in range(4):
+        tt(piece("BC", k, 64), IX(R("c1w"), lst("cc", 576 + k * 48)), piece("BC", k, 64), A.add)
+    invert("s", 1, 2)
+    invert("s", 1, 3)
+    rewrap(1)
+
+    def votes(m, k):
+        mm(R("PV%d" % m, 3 - k, 192, 4),
+           [(R("E", 15 - i, 143 - i), R("VB", k * V + i, (k + 1) * V, 16)) for i in range(16)])
+
+    for k in range(4):
+        act(piece("VB", k), piece("BC", k, 64), F.Sign, bias=col("sm", 10))
+        votes(1, k)
+    act(R("PA", 0, V), R("c1w", 0, V), F.Identity, bias=col("sm", 8))
+
+    ts(R("inv", 0, 256), R("A2", 0, 256), 0.25, A.add)
+    for mh in range(4):
+        ts(R("PB", mh * 192, (mh + 1) * 192), R("fui", mh * 384, mh * 384 + 192), 4096.0, A.mult, 1.0, A.add)
+    for u in range(4):
+        tt(R("A1"), IX(R("BC"), lst("inv", u * 64, 64)), R("A1") if u else R("c1w"), A.max)
+        if u == 3:
+            ts(R("inv", 256, 512), R("A2", 256, 512), 0.25, A.add)
+        for k in range(4):
+            tt(R("BE", 2304 + u * 192 + 3 - k, 2304 + (u + 1) * 192, 4), lst("PB", u * 192 + k * 48),
+               lst("fui", u * 384 + 192 + k * 48), A.add, apart=(u + k > 0))
+    for u in range(4):
+        for a in (0, G):
+            tt(R("A1", V + a, V + a + G), IX(R("BC"), lst("inv", 256 + u * 64 + 48 + a // 16, 8)), R("A1", V + a, V + a + G), A.max)
+    x2 = exchange(3, 1, ("A1", V), ("ld", 0))
+    for u in range(4):
+        for a, b in SIDES:
+            tt(R("A1", a, b), IX(R("BC"), lst("inv", 256 + u * 64 + a // 16, 24)), R("A1", a, b), A.max)
+    for n in range(3):
+        dma("y", [(R("W%d" % n, 0, 4 * W), R("W3", 0, 4 * W))], after=[x2])
+    for n in (4, 5):
+        act(R("W%d" % n, 0, 4 * W), R("W3", 0, 4 * W), F.Copy)
+    act(R("A3"), R("topb"), F.Copy, scale=BIG)
+    act(R("PB", 0, V), R("topb"), F.Copy, scale=BIG)
+
+    def merge(name, level, land, f):
+        acc = R(name, 0, V)
+        l1, l2 = lst("sndu", level * 16, 8), lst("sndu", level * 16 + 8, 8)
+        cp(R("tm", 0, G), IX(acc, l1))
+        tt(IX(acc, l1), R("tm", 0, G), R("ld", land, land + G), f)
+        tt(R("tm", G, 2 * G), IX(acc, l2), R("ld", land + G, land + 2 * G), f)
+        cp(IX(acc, l2), R("tm", G, 2 * G))
+
+    merge("A1", 1, 0, A.max)
+
+    tt(R("PA", 0, V), R("PA", 0, V), R("A1", 0, V), A.subtract)
+    for k in range(4):
+        tt(piece("VB", k), piece("BB", k), R("PA", 0, V), A.is_ge)
+        votes(0, k)
+
+    def choose(m):
+        pv = "PV%d" % m
+        pi = R("fui", 576 * m, 576 * m + 192)
+        ts(R(pv, 192, 384), R(pv, 0, 192), 8.0 if m == 0 else 0.0, A.is_ge)
+        tt(R("BC", 1536, 1728), R(pv, 0, 192), R("CC", m * 384, m * 384 + 192), A.is_lt)
+        for h in range(2):
+            a = 2304 + (m * 2 + h) * 192
+            tt(R("BC", h * 192, (h + 1) * 192), R(pv, 192, 384), R("BE", a, a + 192), A.mult)
+        tt(R("PC", V, V + 192), R(pv, 0, 192), R("CC", m * 384 + 192, (m + 1) * 384), A.is_ge)
+        for h in range(2):
+            scan(R("BC", 384 + h * 192, 576 + h * 192), R("BC", 1536, 1728), R("BC", h * 192, (h + 1) * 192))
+        for h in range(2):
+            tt(R("BC", 1152 + h * 192, 1344 + h * 192), R("PC", V, V + 192), R("BC", 383 + h * 192, 575 + h * 192), A.mult)
+        for h in range(2):
+            scan(R("BC", 768 + h * 192, 960 + h * 192), R("BC", 1536, 1728), R("BC", 1152 + h * 192, 1344 + h * 192))
+        ts(pi, R("BC", 387, 1152, 4), -1.0, A.add)
+        ts(R("fui", 192, 384), pi, 12, A.arith_shift_right, 0x13FF, A.bitwise_and)
+        ts(R("fui", 384, 576), pi, W - 1, A.bitwise_and)
+        ts(R("fc", m * 384, (m + 1) * 384), R("fui", 192, 576), float(W), A.min)
+
+    def places(m):
+        pi = R("fui", 576 * m, 576 * m + 192)
+        spare = R("PC", V, V + 192)
+        ts(spare, pi, -8192.0, A.mult)
+        ts(R("cli", 0, 192), pi, 12, A.arith_shift_right)
+        tt(spare, spare, R("DU"), A.min)
+        ts(R("cli", 192, 384), pi, 4 * W - 1, A.bitwise_and)
+        for s in range(2):
+            tt(R("cli", 384 + s * 192, 576 + s * 192), R("cli", s * 192, (s + 1) * 192), spare, A.max)
+        cp(R("fz", m * 384, (m + 1) * 384), R("cli", 384, V))
+
+    choose(0)
+
+    for q in range(4):
+        act(piece("BA", q), IX(R("flw"), lst("fc", q * 48)), F.Copy, scale=col("fwf", q))
+    places(0)
+    for q in range(4):
+        tt(piece("BC", q, 64), IX(R("flw"), lst("fc", 192 + q * 48)), piece("BA", q), A.mult)
+        if q < PE_SUM:
+            for a, b in ((0, 512), (512, V)):
+                mm(R("PA", a, b), [(R("ID"), R("BC", 64 + q * V + a, 64 + q * V + b))], q == 0, q == PE_SUM - 1)
+        if q == 0 and not PE_SUM:
+            act(R("PA", 0, V), piece("BC", 0, 64), F.Copy)
+    join("BC", 64, "i1w", A.add, max(PE_SUM, 1))
+    cp(R("sa"), IX(R("i1w", 0, V), lst("sndu", 16, 16)))
+    exchange(4, -1, ("sa", 0), ("i1w", V))
+    for q in range(4):
+        act(piece("BD", q), IX(R("flw"), lst("fc", 192 + q * 48)), F.Copy, scale=col("fwf", q))
+    choose(1)
+    places(1)
+
+    def target(win, m, s, q):
+        return IX(R(win), lst("fz", m * 384 + s * 192 + q * 48))
+
+    def product(name, q, o):
+        tt(piece(name, q), piece(name, q), o, A.mult)
+
+    def halve(win):
+        if FOLD2:
+            dma("g", [(R(win, u * W, u * W + V), R(win, (u + 2) * W, (u + 2) * W + V)) for u in range(2)], accum_op=A.add)
+        else:
+            dma("g", [(R(win, 0, W + V), R(win, 2 * W, 3 * W + V))], accum_op=A.add)
+
+    PG = R("PV0", 0, 2 * G)
+
+    def ghosts_pe(win, first, last):
+        mm(PG, [(R("ID"), R(win, u * W + V, (u + 1) * W)) for u in range(4)], first, last)
+
+    def add_ghosts(win, out):
+        for u in range(4):
+            for a in (0, G):
+                tt(R(out if out and u == 3 else "PV0", a, a + G), R("PV0", a, a + G),
+                   R(win, u * W + V + a, u * W + V + a + G), A.add)
+
+    def add_own(slices, out, first):
+        todo = list(slices)
+        if first:
+            (w0, u0), (w1, u1) = todo.pop(0), todo.pop(0)
+            for a, b in SIDES:
+                tt(R("PA", a, b), R(w0, u0 * W + a, u0 * W + b), R(w1, u1 * W + a, u1 * W + b), A.add)
+        for n, (w, u) in enumerate(todo):
+            for a, b in SIDES:
+                tt(R(out if out and n == len(todo) - 1 else "PA", a, b), R("PA", a, b), R(w, u * W + a, u * W + b), A.add)
+
+    def halves(w):
+        return [(w, 0), (w, 1)]
+
+    def whole(w):
+        return [(w, u) for u in range(4)]
+
+    oS, oP = R("A3"), R("PB", 0, V)
+
+    def rw(q):
+        ts(piece("BE", q), IX(R("i1w"), lst("fc", 576 + q * 48)), col("fwf", 4 + q), A.mult)
+
+    def edge(q):
+        tt(piece("BC", q, 64), IX(R("i1w"), lst("fc", 576 + q * 48)), piece("BB", q), A.mult)
+
+    for q in RW_S:
+        act(piece("BE", q), IX(R("i1w"), lst("fc", 576 + q * 48)), F.Copy, scale=col("fwf", 4 + q))
+    for q in (0, 1, 2, 3):
+        act(piece("BB", q), IX(R("i1w"), lst("fc", 384 + q * 48)), F.Copy, scale=col("fwf", 4 + q))
+    for q in (0, 2, 1, 3):
+        if q not in RW_S:
+            rw(q)
+    for q in (0, 2, 1, 3):
+        product("BE", q, oP)
+    for q in (0, 2):
+        act(target("W0", 1, 0, q), piece("BE", q), F.Silu)
+    ghosts_pe("W0", True, False)
+    halve("W0")
+    for q in (1, 3):
+        act(target("W2", 1, 0, q), piece("BE", q), F.Silu)
+    tt(target("W1", 1, 1, 0), oS, piece("BB", 0), A.mult)
+    edge(1)
+    tt(target("W1", 1, 1, 2), oS, piece("BB", 2), A.mult)
+    ghosts_pe("W1", False, False)
+    halve("W1")
+    ghosts_pe("W2", False, True)
+    halve("W2")
+    product("BB", 1, oP)
+    edge(3)
+    product("BB", 3, oP)
+    for q in (1, 3):
+        act(target("W3", 1, 1, q), piece("BB", q), F.Silu)
+    edge(0)
+    edge(2)
+    sl = halves("W0") + halves("W1") + whole("W3") + halves("W2")
+    add_own(sl[:PRE_H], None, True)
+    add_ghosts("W3", "sb")
+    exchange(5, 1, ("sb", 0), ("ld", 256))
+    for a, b in ((0, 512), (512, V)):
+        mm(R("PC", a, b), [(R("ID"), R("BC", 64 + q * V + a, 64 + q * V + b)) for q in (1, 3, 0, 2)])
+    act(R("W0", 2 * W, 4 * W), R("W4", 0, 2 * W), F.Copy)
+    iota(R("W1", 2 * W, 4 * W), [[0, 2 * W]], 0, 0)
+    add_own(sl[PRE_H:], "A1", False)
+    for n in (0, 1):
+        act(R("W%d" % n, 0, 2 * W), R("W4", 0, 2 * W), F.Copy)
+    merge("A1", 1, 256, A.add)
+
+    oS = R("A1", 0, V)
+    act(oP, oS, F.Copy)
+    act(R("A2"), R("PC", 0, V), F.Copy)
+    dma("y", [(H("yi"), R("A2"))])
+    product("BD", 0, oS)
+    product("BD", 2, oP)
+    for q in (0, 2):
+        act(target("W4", 0, 0, q), piece("BD", q), F.Silu)
+    ghosts_pe("W4", True, False)
+    halve("W4")
+    tt(target("W5", 0, 1, 0), oS, piece("BA", 0), A.mult)
+    product("BD", 1, oP)
+    product("BD", 3, oP)
+    for q in (1, 3):
+        act(target("W0", 0, 0, q), piece("BD", q), F.Silu)
+    tt(target("W5", 0, 1, 2), oS, piece("BA", 2), A.mult)
+    ghosts_pe("W5", False, False)
+    halve("W5")
+    ghosts_pe("W0", False, True)
+    halve("W0")
+    if NV == 3:
+        product("BA", 3, oP)
+        tt(target("W1", 0, 1, 1), oS, piece("BA", 1), A.mult)
+    else:
+        product("BA", 1, oP)
+        product("BA", 3, oP)
+        act(target("W1", 0, 1, 1), piece("BA", 1), F.Silu)
+    act(target("W1", 0, 1, 3), piece("BA", 3), F.Silu)
+    sl = halves("W4") + halves("W5") + whole("W1") + halves("W0")
+    add_own(sl[:PRE_I], None, True)
+    add_ghosts("W1", None)
+    for a in (0, G):
+        ts(R("sa", a, a + G), R("PV0", a, a + G), 1.0 / BIG, A.mult)
+    exchange(6, 1, ("sa", 0), ("ld", 512))
+    add_own(sl[PRE_I:], None, False)
+    for a, b in SIDES:
+        ts(R("A3", a, b), R("PA", a, b), 1.0 / BIG, A.mult)
+    merge("A3", 0, 512, A.add)
+    dma("y", [(H("yo"), R("A3"))])
+
+    wait("g", list(count.items()))

@@ -5,6 +5,7 @@ V, W, G, KV = 768, 1024, 128, 3072
 WW = 4992
 BIG = 2.0 ** 40
 SIDES = ((0, V // 2), (V // 2, V))
+BANKS = ((0, 512), (512, V))
 f32, bf, i32, u16 = "float32", "bfloat16", "int32", "uint16"
 
 SCRATCH = {}
@@ -17,7 +18,7 @@ for _n, _c, _t in [
     ("ld", 768, f32), ("tm", 256, f32), ("cli", V, i32), ("cui", V, i32), ("fui", 2 * V, i32),
     ("sndi", 32, i32), ("cri", 8, i32), ("thi", 8, i32), ("fwf", 8, f32), ("sm", 16, f32), ("topb", V, bf),
     ("cc", V, u16), ("pl", 384, u16), ("inv", 512, u16), ("fc", V, u16), ("fz", V, u16), ("sndu", 32, u16),
-    ("CC", V, bf), ("DU", 192, f32), ("E", 144, bf), ("ID", 128, f32),
+    ("CC", V + 192, bf), ("DU", 192, f32), ("E", 144, bf), ("ID", 128, f32), ("NI", 128, f32), ("N8", 128, f32),
 ]:
     SCRATCH[_n] = ("sbuf", [128, _c], _t)
 for _n, _c in [("PA", 1024), ("PB", 1024), ("PC", 1024), ("PV0", 512), ("PV1", 512)]:
@@ -25,12 +26,26 @@ for _n, _c in [("PA", 1024), ("PB", 1024), ("PC", 1024), ("PV0", 512), ("PV1", 5
 
 NDMA = 40
 SEMAPHORES = ["v", "s", "p", "c"] + ["d%d" % _i for _i in range(NDMA)] + ["x%d" % _i for _i in range(7)] + ["l%d" % _i for _i in range(7)]
-PE_SUM = 0
+PE_SUM = 2
 EARLY = "v"
-RW_S = (0,)
+LWV = ()
+ORD_H = "vcb"
+ORD_I = "vcb"
+SMASK = True
 PRE_H = 4
 PRE_I = 4
-NV = 3
+CUT = 0
+NVH = 3
+VINV = 2
+LATE = 1
+LATE_FIRST = True
+VGH = False
+ASSIST = False
+PE_C = True
+BCOPY = 2
+PK0 = 0
+PK1 = 4
+PK2 = 4
 FOLD2 = True
 
 
@@ -189,9 +204,8 @@ def rank_program(g, core, T, topo):
     dma("y", [(R("sndi"), H("snd"))])
     dma("s", [(R("cli"), H("cl"))])
     dma("y", [(R("cui"), H("cu"))])
-    dma("g", [(R("topb"), H("top"))])
     dma("y", [(R("cri"), H("cr")), (R("thi", 0, 2), H("th")), (R("fwf"), H("fw"))])
-    dma("y", [(R("flw", 0, V), H("fl")), (R("fui"), H("fu"))])
+    dma("y", [(R("flw", 0, V), H("fl")), (R("fui", 0, V), (T.fu[:, 0:V], [], []))])
     fill(R("W4", 0, W), 0.0)
     fill(R("W4", W, 2 * W), 0.0)
     fill(R("BC", 0, 64), 0.0)
@@ -204,22 +218,11 @@ def rank_program(g, core, T, topo):
     cp(R("sndu"), R("sndi"))
     cp(R("sa"), IX(R("cli"), lst("sndu", 0, 16)))
     x0 = exchange(0, -1, ("sa", 0), ("clw", V))
-    for k in (1, 2, 3):
+    iota(R("ID"), [[0, 128]], 1, 0)
+    iota(piece("BA", 1), [[1, V]], 64 + V, 0)
+    keep(R("ID"), [[-1, 128]], A.is_equal, 0.0, 0, 1)
+    for k in (2, 3):
         iota(piece("BA", k), [[1, V]], 64 + k * V, 0)
-    act(R("sf"), IX(R("flw", 0, V), lst("sndu", 0, 16)), F.Copy)
-    exchange(1, -1, ("sf", 0), ("flw", V))
-    cp(R("clw", 0, V), R("cli"))
-    ts(R("cli", 0, 384), R("cui", 384, V), 4, A.arith_shift_right)
-    ts(R("cli", 384, V), R("cui", 0, 384), W - 1, A.bitwise_and)
-    ts(R("A1", 0, 384), R("cli", 0, 384), -4095.0 / 256.0, A.mult)
-    cp(R("cc", 0, 384), R("cli", 384, V))
-    tt(R("A1", 384, V), R("cui", 384, V), R("A1", 0, 384), A.add)
-    ts(R("pl"), R("A1", 384, V), 256.0, A.mult)
-    cp(R("sm", 0, 8), R("cri"))
-    cp(R("sm", 8, 10), R("thi", 0, 2))
-    ts(col("sm", 10), col("thi", 1), -1.0, A.mult, 0.5, A.add)
-    dma("y", [(R("W5", u * W, (u + 1) * W), R("W3", 0, W)) for u in range(4)], after=[x0])
-    dma("y", [(R("W3", u * W, (u + 1) * W), R("W3", 0, W)) for u in range(1, 4)])
 
     def invert(q, s, k):
         o = IX(R("W%d" % (4 + s), 0, 4 * W), lst("pl", s * 192 + k * 48))
@@ -230,10 +233,44 @@ def rank_program(g, core, T, topo):
 
     def rewrap(s):
         name = "W%d" % (4 + s)
-        dma("y", [(R("A2", s * 256, (s + 1) * 256), (T[name][0:128:18, 0:4 * W], [(name, 0, 4 * W)], []))])
+        dma("y", [(R("ld", (s + 1) * 256, (s + 2) * 256), (T[name][0:128:18, 0:4 * W], [(name, 0, 4 * W)], []))])
 
-    if EARLY:
-        invert(EARLY, 0, 0)
+    def pack(mh, stage):
+        if stage == 0:
+            ts(R("PB", mh * 192, (mh + 1) * 192), R("fui", mh * 384, mh * 384 + 192), 4096.0, A.mult, 1.0, A.add)
+        else:
+            for k in range(4):
+                tt(R("A2", mh * 192 + 3 - k, (mh + 1) * 192, 4), lst("PB", mh * 192 + k * 48),
+                   lst("fui", mh * 384 + 192 + k * 48), A.add, apart=True)
+
+    zs = [R("cui", 384 + s * 192, 576 + s * 192) for s in range(2)]
+    for s in range(2):
+        ts(R("fui", V + s * 192, V + (s + 1) * 192), zs[s], 4, A.arith_shift_right)
+    for s in range(2):
+        ts(R("PB", s * 192, (s + 1) * 192), R("fui", V + s * 192, V + (s + 1) * 192), -4095.0 / 256.0, A.mult)
+    for s in range(2):
+        tt(R("PB", s * 192, (s + 1) * 192), zs[s], R("PB", s * 192, (s + 1) * 192), A.add)
+    for s in range(2):
+        ts(R("pl", s * 192, (s + 1) * 192), R("PB", s * 192, (s + 1) * 192), 256.0, A.mult)
+    dma("y", [(R("fui", V, 2 * V), (T.fu[:, V:2 * V], [], []))])
+    act(R("sf"), IX(R("flw", 0, V), lst("sndu", 0, 16)), F.Copy)
+    if EARLY == "s":
+        invert("s", 0, 0)
+    exchange(1, -1, ("sf", 0), ("flw", V))
+    dma("g", [(R("topb"), H("top"))])
+    cp(R("clw", 0, V), R("cli"))
+    cp(R("sm", 0, 8), R("cri"))
+    ts(R("cli", 384, V), R("cui", 0, 384), W - 1, A.bitwise_and)
+    cp(R("sm", 8, 10), R("thi", 0, 2))
+    ts(R("cli", 0, 384), R("cui", 384, V), W - 1, A.bitwise_and)
+    cp(R("cc", 0, 384), R("cli", 384, V))
+    ts(R("sm", 11, 13), R("thi", 0, 2), -1.0, A.mult, 0.5, A.add)
+    dma("y", [(R("W5", u * W, (u + 1) * W), R("W3", 0, W)) for u in range(4)], after=[x0])
+    if EARLY == "v":
+        invert("v", 0, 0)
+    for stage in (0, 1):
+        for mh in range(PK0):
+            pack(mh, stage)
 
     def join(name, base, out, f, k0):
         for k in range(k0, 4):
@@ -244,56 +281,68 @@ def rank_program(g, core, T, topo):
         act(piece("BB", k), IX(R("clw"), lst("cc", k * 48)), F.Identity, bias=col("sm", k))
     for k in range(4):
         tt(piece("BB", k), IX(R("clw"), lst("cc", 192 + k * 48)), piece("BB", k), A.add)
-    act(R("PA", 0, V), piece("BB", 0), F.Copy)
+    if BCOPY == 1:
+        act(R("PA", 0, V), piece("BB", 0), F.Copy)
+    else:
+        for a, b in BANKS:
+            mm(R("PA", a, b), [(R("ID"), R("BB", a, b))])
     join("BB", 0, "c1w", A.max, 1)
     cp(R("sb"), IX(R("c1w", 0, V), lst("sndu", 16, 16)))
-    exchange(2, -1, ("sb", 0), ("c1w", V))
+    x1 = exchange(2, -1, ("sb", 0), ("c1w", V))
     iota(R("E"), [[0, 144]], 1, 0)
     iota(R("CC", 0, 384), [[0, 384]], 8, 0)
     iota(R("CC", 384, V), [[0, 384]], 0, 0)
-    iota(R("ID"), [[0, 128]], 1, 0)
+    iota(R("NI"), [[0, 128]], -1, 0)
+    iota(R("N8"), [[0, 128]], -8192, 0)
+    iota(R("CC", V, V + 192), [[0, 192]], 8, 0)
     iota(R("DU"), [[0, 4], [16, 48]], 4 * W, 1)
     keep(R("E"), [[1, 144]], A.is_ge, 0.0, 0, -1)
     for n in range(4):
         keep(R("CC", n * 192, (n + 1) * 192), [[0, 48], [1, 4]], A.is_gt, 1e9 if n % 2 else -1e9, 0, 0)
     keep(R("E"), [[-1, 144]], A.is_ge, 0.0, 15, 1)
-    keep(R("ID"), [[-1, 128]], A.is_equal, 0.0, 0, 1)
+    keep(R("NI"), [[-1, 128]], A.is_equal, 0.0, 0, 1)
+    keep(R("N8"), [[-1, 128]], A.is_equal, 0.0, 0, 1)
+    keep(R("CC", V, V + 192), [[0, 48], [1, 4]], A.is_gt, 0.0, 0, 0)
     keep(R("E"), [[0, 9], [1, 16]], A.is_ge, 0.0, -15, 0)
     for k in range(1 if EARLY else 0, 4):
         invert("s", 0, k)
     rewrap(0)
-    ts(R("cli", 0, 384), R("cui", 384, V), W - 1, A.bitwise_and)
-    invert("v", 1, 0)
+    dma("y", [(R("W3", u * W, (u + 1) * W), R("W3", 0, W)) for u in range(1, 4)], after=[x1])
     cp(R("cc", 384, V), R("cli", 0, 384))
-    invert("v", 1, 1)
+    for k in range(VINV):
+        invert("v", 1, k)
+    for stage in (0, 1):
+        for mh in range(PK0, PK1):
+            pack(mh, stage)
 
     for k in range(4):
         act(piece("BC", k, 64), IX(R("c1w"), lst("cc", 384 + k * 48)), F.Identity, bias=col("sm", 4 + k))
     for k in range(4):
         tt(piece("BC", k, 64), IX(R("c1w"), lst("cc", 576 + k * 48)), piece("BC", k, 64), A.add)
-    invert("s", 1, 2)
-    invert("s", 1, 3)
+    for k in range(VINV, 4):
+        invert("s", 1, k)
     rewrap(1)
+    for a, b in BANKS:
+        mm(R("PC", a, b), [(R("ID"), R("BB", 3 * V + a, 3 * V + b)), (R("NI"), R("c1w", a, b))], True, False)
 
     def votes(m, k):
         mm(R("PV%d" % m, 3 - k, 192, 4),
            [(R("E", 15 - i, 143 - i), R("VB", k * V + i, (k + 1) * V, 16)) for i in range(16)])
 
     for k in range(4):
-        act(piece("VB", k), piece("BC", k, 64), F.Sign, bias=col("sm", 10))
+        act(piece("VB", k), piece("BC", k, 64), F.Sign, bias=col("sm", 12))
         votes(1, k)
     act(R("PA", 0, V), R("c1w", 0, V), F.Identity, bias=col("sm", 8))
 
-    ts(R("inv", 0, 256), R("A2", 0, 256), 0.25, A.add)
-    for mh in range(4):
-        ts(R("PB", mh * 192, (mh + 1) * 192), R("fui", mh * 384, mh * 384 + 192), 4096.0, A.mult, 1.0, A.add)
+    ts(R("inv", 0, 256), R("ld", 256, 512), 0.25, A.add)
+    for mh in range(PK1, 4):
+        pack(mh, 0)
     for u in range(4):
-        tt(R("A1"), IX(R("BC"), lst("inv", u * 64, 64)), R("A1") if u else R("c1w"), A.max)
-        if u == 3:
-            ts(R("inv", 256, 512), R("A2", 256, 512), 0.25, A.add)
-        for k in range(4):
-            tt(R("BE", 2304 + u * 192 + 3 - k, 2304 + (u + 1) * 192, 4), lst("PB", u * 192 + k * 48),
-               lst("fui", u * 384 + 192 + k * 48), A.add, apart=(u + k > 0))
+        for a in (0, 512):
+            tt(R("A1", a, a + 512), IX(R("BC"), lst("inv", u * 64 + a // 16, 32)), R("A1" if u else "c1w", a, a + 512), A.max)
+    for mh in range(PK1, PK2):
+        pack(mh, 1)
+    ts(R("inv", 256, 512), R("ld", 512, 768), 0.25, A.add)
     for u in range(4):
         for a in (0, G):
             tt(R("A1", V + a, V + a + G), IX(R("BC"), lst("inv", 256 + u * 64 + 48 + a // 16, 8)), R("A1", V + a, V + a + G), A.max)
@@ -301,12 +350,14 @@ def rank_program(g, core, T, topo):
     for u in range(4):
         for a, b in SIDES:
             tt(R("A1", a, b), IX(R("BC"), lst("inv", 256 + u * 64 + a // 16, 24)), R("A1", a, b), A.max)
+    for mh in range(PK2, 4):
+        pack(mh, 1)
     for n in range(3):
         dma("y", [(R("W%d" % n, 0, 4 * W), R("W3", 0, 4 * W))], after=[x2])
-    for n in (4, 5):
-        act(R("W%d" % n, 0, 4 * W), R("W3", 0, 4 * W), F.Copy)
     act(R("A3"), R("topb"), F.Copy, scale=BIG)
-    act(R("PB", 0, V), R("topb"), F.Copy, scale=BIG)
+    for q in range(4):
+        act(piece("BE", q), R("A3"), F.Copy, scale=col("fwf", 4 + q))
+    act(R("W4", 0, 2 * W), R("W3", 0, 2 * W), F.Copy)
 
     def merge(name, level, land, f):
         acc = R(name, 0, V)
@@ -318,37 +369,61 @@ def rank_program(g, core, T, topo):
 
     merge("A1", 1, 0, A.max)
 
-    tt(R("PA", 0, V), R("PA", 0, V), R("A1", 0, V), A.subtract)
-    for k in range(4):
-        tt(piece("VB", k), piece("BB", k), R("PA", 0, V), A.is_ge)
+    for a, b in BANKS:
+        mm(R("PC", a, b), [(R("ID"), R("A1", a, b))], False, True)
+    act(piece("VB", 3), R("PC", 0, V), F.Sign, bias=col("sm", 11))
+    if SMASK:
+        act(R("tm", 0, 192), R("PV1", 0, 192), F.Sign, bias=1.0)
+        act(R("PV1", 192, 384), R("tm", 0, 192), F.Relu)
+        act(R("PV1", 0, 192), R("tm", 0, 192), F.Relu)
+        act(R("tm", 0, 192), R("tm", 0, 192), F.Relu, scale=-1.0)
+        act(R("PV1", 0, 192, 4), R("PV1", 0, 192, 4), F.Copy, scale=0.0)
+        act(R("tm", 0, 192, 4), R("tm", 0, 192, 4), F.Copy, scale=0.0)
+    act(R("PB", 0, V), R("topb"), F.Copy, scale=BIG)
+    act(R("W4", 2 * W, 4 * W), R("W3", 2 * W, 4 * W), F.Copy)
+    iota(R("W5", 0, 2 * W), [[0, 2 * W]], 0, 0)
+    for a, b in SIDES:
+        tt(R("PA", a, b), R("PA", a, b), R("A1", a, b), A.subtract)
+    for k in range(3):
+        for a, b in SIDES if k == 0 else ((0, V),):
+            tt(R("VB", k * V + a, k * V + b), R("BB", k * V + a, k * V + b), R("PA", a, b), A.is_ge)
         votes(0, k)
+        if k == 1:
+            votes(0, 3)
 
     def choose(m):
         pv = "PV%d" % m
         pi = R("fui", 576 * m, 576 * m + 192)
-        ts(R(pv, 192, 384), R(pv, 0, 192), 8.0 if m == 0 else 0.0, A.is_ge)
-        tt(R("BC", 1536, 1728), R(pv, 0, 192), R("CC", m * 384, m * 384 + 192), A.is_lt)
+        dead, later = R("BC", 1536, 1728), R("PC", V, V + 192)
+        if m == 0:
+            tt(R(pv, 192, 384), R(pv, 0, 192), R("CC", V, V + 192), A.is_ge)
+        elif not SMASK:
+            ts(R(pv, 192, 384), R(pv, 0, 192), 0.0, A.is_ge)
+        if m == 1 and SMASK:
+            dead, later = R("tm", 0, 192), R(pv, 0, 192)
+        else:
+            tt(dead, R(pv, 0, 192), R("CC", m * 384, m * 384 + 192), A.is_lt)
         for h in range(2):
-            a = 2304 + (m * 2 + h) * 192
-            tt(R("BC", h * 192, (h + 1) * 192), R(pv, 192, 384), R("BE", a, a + 192), A.mult)
-        tt(R("PC", V, V + 192), R(pv, 0, 192), R("CC", m * 384 + 192, (m + 1) * 384), A.is_ge)
+            a = (m * 2 + h) * 192
+            tt(R("BC", h * 192, (h + 1) * 192), R(pv, 192, 384), R("A2", a, a + 192), A.mult)
+        if m == 0 or not SMASK:
+            tt(later, R(pv, 0, 192), R("CC", m * 384 + 192, (m + 1) * 384), A.is_ge)
         for h in range(2):
-            scan(R("BC", 384 + h * 192, 576 + h * 192), R("BC", 1536, 1728), R("BC", h * 192, (h + 1) * 192))
+            scan(R("BC", 384 + h * 192, 576 + h * 192), dead, R("BC", h * 192, (h + 1) * 192))
         for h in range(2):
-            tt(R("BC", 1152 + h * 192, 1344 + h * 192), R("PC", V, V + 192), R("BC", 383 + h * 192, 575 + h * 192), A.mult)
+            tt(R("BC", 1152 + h * 192, 1344 + h * 192), later, R("BC", 383 + h * 192, 575 + h * 192), A.mult)
         for h in range(2):
-            scan(R("BC", 768 + h * 192, 960 + h * 192), R("BC", 1536, 1728), R("BC", 1152 + h * 192, 1344 + h * 192))
+            scan(R("BC", 768 + h * 192, 960 + h * 192), dead, R("BC", 1152 + h * 192, 1344 + h * 192))
         ts(pi, R("BC", 387, 1152, 4), -1.0, A.add)
+        mm(R(pv, 0, 192), [(R("ID"), R("DU")), (R("N8"), R("BC", 387, 1152, 4))])
         ts(R("fui", 192, 384), pi, 12, A.arith_shift_right, 0x13FF, A.bitwise_and)
         ts(R("fui", 384, 576), pi, W - 1, A.bitwise_and)
         ts(R("fc", m * 384, (m + 1) * 384), R("fui", 192, 576), float(W), A.min)
 
     def places(m):
         pi = R("fui", 576 * m, 576 * m + 192)
-        spare = R("PC", V, V + 192)
-        ts(spare, pi, -8192.0, A.mult)
+        spare = R("PV%d" % m, 0, 192)
         ts(R("cli", 0, 192), pi, 12, A.arith_shift_right)
-        tt(spare, spare, R("DU"), A.min)
         ts(R("cli", 192, 384), pi, 4 * W - 1, A.bitwise_and)
         for s in range(2):
             tt(R("cli", 384 + s * 192, 576 + s * 192), R("cli", s * 192, (s + 1) * 192), spare, A.max)
@@ -371,6 +446,7 @@ def rank_program(g, core, T, topo):
     exchange(4, -1, ("sa", 0), ("i1w", V))
     for q in range(4):
         act(piece("BD", q), IX(R("flw"), lst("fc", 192 + q * 48)), F.Copy, scale=col("fwf", q))
+    act(R("W5", 2 * W, 4 * W), R("W3", 2 * W, 4 * W), F.Copy)
     choose(1)
     places(1)
 
@@ -391,20 +467,29 @@ def rank_program(g, core, T, topo):
     def ghosts_pe(win, first, last):
         mm(PG, [(R("ID"), R(win, u * W + V, (u + 1) * W)) for u in range(4)], first, last)
 
-    def add_ghosts(win, out):
-        for u in range(4):
+    def last_ghosts(win, out, scale=None):
+        if not VGH:
+            ghosts_pe(win, False, True)
+            act(R(out), PG, F.Copy, scale=scale or 1.0)
+            return
+        mm(PG, [(R("ID"), R(win, u * W + V, (u + 1) * W)) for u in range(2)], False, True)
+        tt(R("tm"), R(win, 2 * W + V, 3 * W), R(win, 3 * W + V, 4 * W), A.add)
+        if scale is None:
+            tt(R(out), PG, R("tm"), A.add)
+        else:
             for a in (0, G):
-                tt(R(out if out and u == 3 else "PV0", a, a + G), R("PV0", a, a + G),
-                   R(win, u * W + V + a, u * W + V + a + G), A.add)
+                tt(R("PV0", a, a + G), R("PV0", a, a + G), R("tm", a, a + G), A.add)
+            for a in (0, G):
+                ts(R(out, a, a + G), R("PV0", a, a + G), scale, A.mult)
 
-    def add_own(slices, out, first):
+    def add_own(slices, out, first, sides=SIDES):
         todo = list(slices)
         if first:
             (w0, u0), (w1, u1) = todo.pop(0), todo.pop(0)
-            for a, b in SIDES:
+            for a, b in sides:
                 tt(R("PA", a, b), R(w0, u0 * W + a, u0 * W + b), R(w1, u1 * W + a, u1 * W + b), A.add)
         for n, (w, u) in enumerate(todo):
-            for a, b in SIDES:
+            for a, b in sides:
                 tt(R(out if out and n == len(todo) - 1 else "PA", a, b), R("PA", a, b), R(w, u * W + a, u * W + b), A.add)
 
     def halves(w):
@@ -415,21 +500,16 @@ def rank_program(g, core, T, topo):
 
     oS, oP = R("A3"), R("PB", 0, V)
 
-    def rw(q):
-        ts(piece("BE", q), IX(R("i1w"), lst("fc", 576 + q * 48)), col("fwf", 4 + q), A.mult)
-
     def edge(q):
         tt(piece("BC", q, 64), IX(R("i1w"), lst("fc", 576 + q * 48)), piece("BB", q), A.mult)
 
-    for q in RW_S:
-        act(piece("BE", q), IX(R("i1w"), lst("fc", 576 + q * 48)), F.Copy, scale=col("fwf", 4 + q))
-    for q in (0, 1, 2, 3):
-        act(piece("BB", q), IX(R("i1w"), lst("fc", 384 + q * 48)), F.Copy, scale=col("fwf", 4 + q))
     for q in (0, 2, 1, 3):
-        if q not in RW_S:
-            rw(q)
+        if q not in LWV:
+            act(piece("BB", q), IX(R("i1w"), lst("fc", 384 + q * 48)), F.Copy, scale=col("fwf", 4 + q))
     for q in (0, 2, 1, 3):
-        product("BE", q, oP)
+        tt(piece("BE", q), IX(R("i1w"), lst("fc", 576 + q * 48)), piece("BE", q), A.mult)
+    for q in LWV:
+        ts(piece("BB", q), IX(R("i1w"), lst("fc", 384 + q * 48)), col("fwf", 4 + q), A.mult)
     for q in (0, 2):
         act(target("W0", 1, 0, q), piece("BE", q), F.Silu)
     ghosts_pe("W0", True, False)
@@ -437,40 +517,57 @@ def rank_program(g, core, T, topo):
     for q in (1, 3):
         act(target("W2", 1, 0, q), piece("BE", q), F.Silu)
     tt(target("W1", 1, 1, 0), oS, piece("BB", 0), A.mult)
-    edge(1)
     tt(target("W1", 1, 1, 2), oS, piece("BB", 2), A.mult)
     ghosts_pe("W1", False, False)
     halve("W1")
-    ghosts_pe("W2", False, True)
+    ghosts_pe("W2", False, False)
     halve("W2")
-    product("BB", 1, oP)
-    edge(3)
-    product("BB", 3, oP)
-    for q in (1, 3):
-        act(target("W3", 1, 1, q), piece("BB", q), F.Silu)
-    edge(0)
-    edge(2)
-    sl = halves("W0") + halves("W1") + whole("W3") + halves("W2")
-    add_own(sl[:PRE_H], None, True)
-    add_ghosts("W3", "sb")
+    if NVH == 2:
+        edge(1)
+        product("BB", 1, oP)
+        edge(3)
+        product("BB", 3, oP)
+        act(target("W3", 1, 1, 1), piece("BB", 1), F.Silu)
+    else:
+        tt(target("W3", 1, 1, 1), oS, piece("BB", 1), A.mult)
+        if NVH == 4:
+            tt(target("W3", 1, 1, 3), oS, piece("BB", 3), A.mult)
+        edge(3)
+        if NVH == 3:
+            product("BB", 3, oP)
+    if NVH < 4:
+        act(target("W3", 1, 1, 3), piece("BB", 3), F.Silu)
+    order = (3, 1, 0, 2)
+    for q in order[NVH == 2 and 2 or 1:4 - LATE]:
+        edge(q)
+    add_own(halves("W0"), None, True)
+    last_ghosts("W3", "sb")
     exchange(5, 1, ("sb", 0), ("ld", 256))
-    for a, b in ((0, 512), (512, V)):
-        mm(R("PC", a, b), [(R("ID"), R("BC", 64 + q * V + a, 64 + q * V + b)) for q in (1, 3, 0, 2)])
+
+    def sum_edges(qs, first, last):
+        for a, b in BANKS:
+            mm(R("PC", a, b), [(R("ID"), R("BC", 64 + q * V + a, 64 + q * V + b)) for q in qs], first, last)
+        if last:
+            act(R("A2"), R("PC", 0, V), F.Copy)
+            dma("y", [(H("yi"), R("A2"))])
+
     act(R("W0", 2 * W, 4 * W), R("W4", 0, 2 * W), F.Copy)
     iota(R("W1", 2 * W, 4 * W), [[0, 2 * W]], 0, 0)
-    add_own(sl[PRE_H:], "A1", False)
+    parts = {"v": halves("W1"), "c": whole("W3"), "b": halves("W2")}
+    add_own([x for n in ORD_H for x in parts[n]], "A1", False)
     for n in (0, 1):
         act(R("W%d" % n, 0, 2 * W), R("W4", 0, 2 * W), F.Copy)
     merge("A1", 1, 256, A.add)
 
     oS = R("A1", 0, V)
     act(oP, oS, F.Copy)
-    act(R("A2"), R("PC", 0, V), F.Copy)
-    dma("y", [(H("yi"), R("A2"))])
-    product("BD", 0, oS)
+    for a, b in SIDES:
+        tt(R("BD", a, b), R("BD", a, b), R("A1", a, b), A.mult)
     product("BD", 2, oP)
-    for q in (0, 2):
-        act(target("W4", 0, 0, q), piece("BD", q), F.Silu)
+    sum_edges(order[:4 - LATE], True, not LATE)
+    for a, b in SIDES:
+        act(IX(R("W4"), lst("fz", a // 16, 24)), R("BD", a, b), F.Silu)
+    act(target("W4", 0, 0, 2), piece("BD", 2), F.Silu)
     ghosts_pe("W4", True, False)
     halve("W4")
     tt(target("W5", 0, 1, 0), oS, piece("BA", 0), A.mult)
@@ -481,25 +578,28 @@ def rank_program(g, core, T, topo):
     tt(target("W5", 0, 1, 2), oS, piece("BA", 2), A.mult)
     ghosts_pe("W5", False, False)
     halve("W5")
-    ghosts_pe("W0", False, True)
+    ghosts_pe("W0", False, False)
     halve("W0")
-    if NV == 3:
-        product("BA", 3, oP)
-        tt(target("W1", 0, 1, 1), oS, piece("BA", 1), A.mult)
-    else:
-        product("BA", 1, oP)
-        product("BA", 3, oP)
-        act(target("W1", 0, 1, 1), piece("BA", 1), F.Silu)
-    act(target("W1", 0, 1, 3), piece("BA", 3), F.Silu)
-    sl = halves("W4") + halves("W5") + whole("W1") + halves("W0")
-    add_own(sl[:PRE_I], None, True)
-    add_ghosts("W1", None)
-    for a in (0, G):
-        ts(R("sa", a, a + G), R("PV0", a, a + G), 1.0 / BIG, A.mult)
+    cut = 3 * V + CUT
+    tt(R("BA", cut, 4 * V), R("BA", cut, 4 * V), R("PB", CUT, V), A.mult)
+    tt(target("W1", 0, 1, 1), oS, piece("BA", 1), A.mult)
+    if CUT:
+        tt(IX(R("W1"), lst("fz", 336, CUT // 16)), R("A1", 0, CUT), R("BA", 3 * V, cut), A.mult)
+    act(IX(R("W1"), lst("fz", 336 + CUT // 16, (V - CUT) // 16)), R("BA", cut, 4 * V), F.Silu)
+    for q in order[4 - LATE:]:
+        edge(q)
+    add_own(halves("W4"), None, True, BANKS[::-1])
+    last_ghosts("W1", "sa", 1.0 / BIG)
     exchange(6, 1, ("sa", 0), ("ld", 512))
-    add_own(sl[PRE_I:], None, False)
-    for a, b in SIDES:
-        ts(R("A3", a, b), R("PA", a, b), 1.0 / BIG, A.mult)
+    parts = {"v": halves("W5"), "c": whole("W1"), "b": halves("W0")}
+    add_own([x for n in ORD_I for x in parts[n]], None, False, BANKS[::-1])
+    act(R("A3", 512, V), R("PA", 512, V), F.Copy, scale=1.0 / BIG)
+    ts(R("A3", 0, 512), R("PA", 0, 512), 1.0 / BIG, A.mult)
+    if not LATE_FIRST:
+        for q in order[4 - LATE:]:
+            edge(q)
+    if LATE:
+        sum_edges(order[4 - LATE:], False, True)
     merge("A3", 0, 512, A.add)
     dma("y", [(H("yo"), R("A3"))])
 

@@ -2,51 +2,57 @@ from concourse.bass import DstId, RemoteDMATransfer
 from concourse.mybir import AluOpType as A, ActivationFunctionType as F
 
 V, W, G, KV = 768, 1024, 128, 3072
-WW = 4992
+U = 4 * W
+STRIP = V + G
+LD = 8 + 2 * G
 BIG = 2.0 ** 40
 SIDES = ((0, V // 2), (V // 2, V))
-BANKS = ((0, 512), (512, V))
 f32, bf, i32, u16 = "float32", "bfloat16", "int32", "uint16"
 
 SCRATCH = {}
-for _n in range(6):
-    SCRATCH["W%d" % _n] = ("sbuf", [128, WW], f32)
 for _n, _c, _t in [
-    ("BA", KV, f32), ("BB", KV, f32), ("BC", KV + 64, f32), ("BD", KV, f32), ("BE", KV, f32),
-    ("VB", KV, bf), ("clw", W, f32), ("c1w", W, f32), ("flw", W + 16, bf), ("i1w", W + 16, f32),
-    ("A1", W, f32), ("A2", V, f32), ("A3", V, f32), ("sa", 256, f32), ("sb", 256, f32), ("sf", 256, bf),
-    ("ld", 768, f32), ("tm", 256, f32), ("cli", V, i32), ("cui", V, i32), ("fui", 2 * V, i32),
+    ("WW", 8 * U + STRIP, f32), ("BA", KV, f32), ("BB", KV, f32), ("BC", KV + 64, f32), ("BE", KV, f32),
+    ("VB", 2 * KV, bf), ("A1", W, f32), ("c1w", W, f32), ("flw", W + 16, bf), ("i1w", W + 16, f32),
+    ("A2", V, f32), ("A3", V, f32), ("sa", 256, f32), ("sf", 256, bf),
+    ("ld", 3 * LD, f32), ("tm", 192, f32), ("cli", V, i32), ("fui", 2 * V + 32, i32), ("blk", 32, i32),
     ("sndi", 32, i32), ("cri", 8, i32), ("thi", 8, i32), ("fwf", 8, f32), ("sm", 16, f32), ("topb", V, bf),
-    ("cc", V, u16), ("pl", 384, u16), ("inv", 512, u16), ("fc", V, u16), ("fz", V, u16), ("sndu", 32, u16),
-    ("CC", V + 192, bf), ("DU", 192, f32), ("E", 144, bf), ("ID", 128, f32), ("NI", 128, f32), ("N8", 128, f32),
+    ("cc", V, u16), ("pl", 416, u16), ("inv", 768, u16), ("fc", V, u16), ("fz", V, u16), ("sndu", 32, u16),
+    ("CC", 576, bf), ("DU", 192, f32), ("E", 144, bf), ("ID", 128, f32), ("NI", 128, f32), ("N8", 128, f32),
 ]:
     SCRATCH[_n] = ("sbuf", [128, _c], _t)
-for _n, _c in [("PA", 1024), ("PB", 1024), ("PC", 1024), ("PV0", 512), ("PV1", 512)]:
-    SCRATCH[_n] = ("psum", [128, _c], f32)
+SCRATCH["PS"] = ("psum", [128, 4096], f32)
 
-NDMA = 40
+NDMA = 48
 SEMAPHORES = ["v", "s", "p", "c"] + ["d%d" % _i for _i in range(NDMA)] + ["x%d" % _i for _i in range(7)] + ["l%d" % _i for _i in range(7)]
+PR3 = True
+YG, YO = 4, 2
+XB = 0
 PE_SUM = 2
-EARLY = "v"
-LWV = ()
-ORD_H = "vcb"
-ORD_I = "vcb"
-SMASK = True
-PRE_H = 4
-PRE_I = 4
-CUT = 0
-NVH = 3
-VINV = 2
-LATE = 1
-LATE_FIRST = True
-VGH = False
-ASSIST = False
-PE_C = True
-BCOPY = 2
-PK0 = 0
-PK1 = 4
-PK2 = 4
-FOLD2 = True
+YIN = 3
+C1T = "late"
+PLAN2 = (0, 1, 3, False, 0, "raw")
+PLAN1 = (2, 0, 2, False, 0, "raw")
+GH2 = ("raw", "raw")
+GH1 = ("raw", "raw")
+OP = "pre"
+JS = 0
+YS = "d"
+BDE = 1
+V1 = 4
+ONE = False
+HALF = 0
+DG = "v"
+ZERO = ((1,), (), (4, 5, 7), ())
+GZERO = (2, 3, 6)
+GZ = (4, 0)
+SA, VA = 1280, 1152
+PKS = ((), (0, 1), (), (2, 3))
+LAT = 200
+LATEC = 4
+SKIPW = False
+HS = (False, False, True)
+INVC = (("s", 0, 256), "snd", ("s", 1, KV), ("v", 0, KV), "pack")
+CUT2, CUT1 = 256, 128
 
 
 def rank_program(g, core, T, topo):
@@ -67,10 +73,8 @@ def rank_program(g, core, T, topo):
     def IX(win, off):
         return (win[0].indirect(off[0]), win[1], off[1])
 
-    def span(name, a, b):
-        if SCRATCH[name][0] == "psum":
-            return a // 512 * 512, -(-b // 512) * 512
-        return a, b
+    def span(a, b):
+        return a // 512 * 512, -(-b // 512) * 512
 
     def wait(q, tickets):
         need = {}
@@ -89,12 +93,12 @@ def rank_program(g, core, T, topo):
                 for a2, b2, w2, q2, tk in log.get(name, []):
                     mine = compute and q2 == q
                     if ps and not mine:
-                        lo, hi = span(name, a, b)
-                        lo2, hi2 = span(name, a2, b2)
+                        lo, hi = span(a, b)
+                        lo2, hi2 = span(a2, b2)
                         if lo < hi2 and lo2 < hi:
                             res.append(tk)
                     elif a < b2 and a2 < b and (w2 or isw):
-                        if mine and isw and q == "p":
+                        if mine and isw and (q == "p" or (SKIPW and w2 and name == "WW")):
                             continue
                         res.append(tk)
         return res
@@ -104,7 +108,52 @@ def rank_program(g, core, T, topo):
             for name, a, b in regs:
                 log.setdefault(name, []).append((a, b, isw, q, tk))
 
+    held = []
+
+    def hold(f, *args):
+        held.append([])
+        f(*args)
+        return held.pop()
+
+    def weave(main, spare):
+        now, past, spare = 0, [], list(spare)
+
+        def touch(c):
+            return [(r, True) for o in c[1] for r in o[1]] + [(r, False) for o in c[1] for r in o[2]] + \
+                   [(r, False) for x in c[2] for r in x[1] + x[2]]
+
+        def ready(c):
+            return max([0] + [end + LAT for end, d in past for (n, a, b), w in touch(c) for (n2, a2, b2), w2 in touch(d)
+                              if n == n2 and a < b2 and a2 < b and (w2 or w) and not (c[4] and w and w2)])
+
+        def issue(c, start):
+            op(*c)
+            o = c[1][0]
+            n = (o[2][0][2] - o[2][0][1]) * 40 if o[2] else max(64, o[0].shape[1])
+            past.append((start + n, c))
+            return start + n
+
+        for c in main:
+            if isinstance(c, int):
+                until = now + c
+            elif c[0] != "v":
+                op(*c)
+                continue
+            else:
+                until = ready(c)
+            while spare and now + 32 < until and (spare[0][0] != "v" or ready(spare[0]) < until):
+                if spare[0][0] != "v":
+                    op(*spare.pop(0))
+                else:
+                    now = issue(spare[0], max(now, ready(spare[0])))
+                    spare.pop(0)
+            now = max(now, until) if isinstance(c, int) else issue(c, max(now, until))
+        return spare
+
     def op(q, outs, ins, emit, apart=False):
+        if held:
+            held[-1].append((q, outs, ins, emit, apart))
+            return
         writes = [r for o in outs for r in o[1]]
         reads = [r for o in outs for r in o[2]] + [r for x in ins for r in x[1] + x[2]]
         wait(q, deps(q, reads, [] if apart else writes, True))
@@ -192,6 +241,16 @@ def rank_program(g, core, T, topo):
             return ins
         op("p", [o], [x for t in terms for x in t], emit)
 
+    def pe(at, n, terms, first=True, last=True):
+        a = at
+        while a < at + n:
+            b = min(at + n, a // 512 * 512 + 512)
+            mm(P(a, b), [(R(l), R(name, c + a - at, c + b - at)) for l, name, c in terms], first, last)
+            a = b
+
+    def P(a, b, step=1):
+        return R("PS", a, b, step)
+
     def piece(name, k, base=0):
         return R(name, base + k * V, base + (k + 1) * V)
 
@@ -201,406 +260,512 @@ def rank_program(g, core, T, topo):
     def col(name, a):
         return R(name, a, a + 1)
 
+    def zero(wins, after):
+        for n in wins:
+            dma("y", [(R("WW", n * U, (n + 1) * U), R("WW", 0, U))], after=[after])
+
+    PD, PM, PT = 0, KV, 2560
+    INV = (5 * U, 7 * U, 3 * U)
+
+    def few(s):
+        return (T.WW[0:128:18, INV[s]:INV[s] + U], [("WW", INV[s], INV[s] + U)], [])
+
     dma("y", [(R("sndi"), H("snd"))])
     dma("s", [(R("cli"), H("cl"))])
-    dma("y", [(R("cui"), H("cu"))])
+    dma("y", [(R("fui", V, 2 * V), H("cu"))])
+    fill(R("WW", 0, 256), 0.0)
+    fill(R("WW", 256, W), 0.0)
+    fill(R("WW", W, 2 * W), 0.0)
+    dma("y", [(few(0), R("WW", 0, 256))])
     dma("y", [(R("cri"), H("cr")), (R("thi", 0, 2), H("th")), (R("fwf"), H("fw"))])
-    dma("y", [(R("flw", 0, V), H("fl")), (R("fui", 0, V), (T.fu[:, 0:V], [], []))])
-    fill(R("W4", 0, W), 0.0)
-    fill(R("W4", W, 2 * W), 0.0)
+    dma("y", [(few(s), R("WW", 0, 256)) for s in (2, 1)])
     fill(R("BC", 0, 64), 0.0)
+    for n in range(3):
+        fill(R("ld", n * LD, n * LD + 8), 0.0)
+    iota(R("blk"), [[W, 4], [0, 8]], 0, 0)
     fill(R("flw", W, W + 16), 0.0)
     fill(R("i1w", W, W + 16), 0.0)
-    act(R("W4", 2 * W, 3 * W), R("W4", 0, W), F.Copy)
-    act(R("W4", 3 * W, 4 * W), R("W4", 0, W), F.Copy)
-    act(R("W3", 0, W), R("W4", 0, W), F.Copy)
-    iota(piece("BA", 0), [[1, V]], 64, 0)
+    for u in (2, 3):
+        act(R("WW", u * W, (u + 1) * W), R("WW", 0, W), F.Silu)
+    for k in (0, 1):
+        iota(piece("BA", k), [[1, V]], 64 + k * V, 0)
     cp(R("sndu"), R("sndi"))
+    tt(R("fui", 2 * V, 2 * V + 32), R("sndi"), R("blk"), A.add)
     cp(R("sa"), IX(R("cli"), lst("sndu", 0, 16)))
-    x0 = exchange(0, -1, ("sa", 0), ("clw", V))
+    x0 = exchange(0, -1, ("sa", 0), ("A1", V))
     iota(R("ID"), [[0, 128]], 1, 0)
-    iota(piece("BA", 1), [[1, V]], 64 + V, 0)
+    iota(R("NI"), [[0, 128]], -1, 0)
     keep(R("ID"), [[-1, 128]], A.is_equal, 0.0, 0, 1)
+    keep(R("NI"), [[-1, 128]], A.is_equal, 0.0, 0, 1)
     for k in (2, 3):
         iota(piece("BA", k), [[1, V]], 64 + k * V, 0)
-
-    def invert(q, s, k):
-        o = IX(R("W%d" % (4 + s), 0, 4 * W), lst("pl", s * 192 + k * 48))
-        if q == "s":
-            act(o, piece("BA", k), F.Silu)
-        else:
-            cp(o, piece("BA", k))
-
-    def rewrap(s):
-        name = "W%d" % (4 + s)
-        dma("y", [(R("ld", (s + 1) * 256, (s + 2) * 256), (T[name][0:128:18, 0:4 * W], [(name, 0, 4 * W)], []))])
-
-    def pack(mh, stage):
-        if stage == 0:
-            ts(R("PB", mh * 192, (mh + 1) * 192), R("fui", mh * 384, mh * 384 + 192), 4096.0, A.mult, 1.0, A.add)
-        else:
-            for k in range(4):
-                tt(R("A2", mh * 192 + 3 - k, (mh + 1) * 192, 4), lst("PB", mh * 192 + k * 48),
-                   lst("fui", mh * 384 + 192 + k * 48), A.add, apart=True)
-
-    zs = [R("cui", 384 + s * 192, 576 + s * 192) for s in range(2)]
-    for s in range(2):
-        ts(R("fui", V + s * 192, V + (s + 1) * 192), zs[s], 4, A.arith_shift_right)
-    for s in range(2):
-        ts(R("PB", s * 192, (s + 1) * 192), R("fui", V + s * 192, V + (s + 1) * 192), -4095.0 / 256.0, A.mult)
-    for s in range(2):
-        tt(R("PB", s * 192, (s + 1) * 192), zs[s], R("PB", s * 192, (s + 1) * 192), A.add)
-    for s in range(2):
-        ts(R("pl", s * 192, (s + 1) * 192), R("PB", s * 192, (s + 1) * 192), 256.0, A.mult)
-    dma("y", [(R("fui", V, 2 * V), (T.fu[:, V:2 * V], [], []))])
-    act(R("sf"), IX(R("flw", 0, V), lst("sndu", 0, 16)), F.Copy)
-    if EARLY == "s":
-        invert("s", 0, 0)
-    exchange(1, -1, ("sf", 0), ("flw", V))
     dma("g", [(R("topb"), H("top"))])
-    cp(R("clw", 0, V), R("cli"))
-    cp(R("sm", 0, 8), R("cri"))
-    ts(R("cli", 384, V), R("cui", 0, 384), W - 1, A.bitwise_and)
-    cp(R("sm", 8, 10), R("thi", 0, 2))
-    ts(R("cli", 0, 384), R("cui", 384, V), W - 1, A.bitwise_and)
-    cp(R("cc", 0, 384), R("cli", 384, V))
-    ts(R("sm", 11, 13), R("thi", 0, 2), -1.0, A.mult, 0.5, A.add)
-    dma("y", [(R("W5", u * W, (u + 1) * W), R("W3", 0, W)) for u in range(4)], after=[x0])
-    if EARLY == "v":
-        invert("v", 0, 0)
-    for stage in (0, 1):
-        for mh in range(PK0):
-            pack(mh, stage)
 
-    def join(name, base, out, f, k0):
-        for k in range(k0, 4):
-            for a, b in SIDES:
-                tt(R(out if k == 3 else "PA", a, b), R("PA", a, b), R(name, base + k * V + a, base + k * V + b), f)
-
-    for k in range(4):
-        act(piece("BB", k), IX(R("clw"), lst("cc", k * 48)), F.Identity, bias=col("sm", k))
-    for k in range(4):
-        tt(piece("BB", k), IX(R("clw"), lst("cc", 192 + k * 48)), piece("BB", k), A.add)
-    if BCOPY == 1:
-        act(R("PA", 0, V), piece("BB", 0), F.Copy)
-    else:
-        for a, b in BANKS:
-            mm(R("PA", a, b), [(R("ID"), R("BB", a, b))])
-    join("BB", 0, "c1w", A.max, 1)
-    cp(R("sb"), IX(R("c1w", 0, V), lst("sndu", 16, 16)))
-    x1 = exchange(2, -1, ("sb", 0), ("c1w", V))
     iota(R("E"), [[0, 144]], 1, 0)
     iota(R("CC", 0, 384), [[0, 384]], 8, 0)
-    iota(R("CC", 384, V), [[0, 384]], 0, 0)
-    iota(R("NI"), [[0, 128]], -1, 0)
+    iota(R("CC", 384, 576), [[0, 192]], 8, 0)
     iota(R("N8"), [[0, 128]], -8192, 0)
-    iota(R("CC", V, V + 192), [[0, 192]], 8, 0)
-    iota(R("DU"), [[0, 4], [16, 48]], 4 * W, 1)
+    iota(R("DU"), [[0, 4], [16, 48]], U, 1)
     keep(R("E"), [[1, 144]], A.is_ge, 0.0, 0, -1)
-    for n in range(4):
+    for n in range(2):
         keep(R("CC", n * 192, (n + 1) * 192), [[0, 48], [1, 4]], A.is_gt, 1e9 if n % 2 else -1e9, 0, 0)
     keep(R("E"), [[-1, 144]], A.is_ge, 0.0, 15, 1)
-    keep(R("NI"), [[-1, 128]], A.is_equal, 0.0, 0, 1)
     keep(R("N8"), [[-1, 128]], A.is_equal, 0.0, 0, 1)
-    keep(R("CC", V, V + 192), [[0, 48], [1, 4]], A.is_gt, 0.0, 0, 0)
+    if XB:
+        keep(R("CC", 448, 576), [[0, 32], [1, 4]], A.is_gt, 0.0, 0, 0)
     keep(R("E"), [[0, 9], [1, 16]], A.is_ge, 0.0, -15, 0)
-    for k in range(1 if EARLY else 0, 4):
-        invert("s", 0, k)
-    rewrap(0)
-    dma("y", [(R("W3", u * W, (u + 1) * W), R("W3", 0, W)) for u in range(1, 4)], after=[x1])
-    cp(R("cc", 384, V), R("cli", 0, 384))
-    for k in range(VINV):
-        invert("v", 1, k)
-    for stage in (0, 1):
-        for mh in range(PK0, PK1):
-            pack(mh, stage)
 
-    for k in range(4):
-        act(piece("BC", k, 64), IX(R("c1w"), lst("cc", 384 + k * 48)), F.Identity, bias=col("sm", 4 + k))
-    for k in range(4):
-        tt(piece("BC", k, 64), IX(R("c1w"), lst("cc", 576 + k * 48)), piece("BC", k, 64), A.add)
-    for k in range(VINV, 4):
-        invert("s", 1, k)
-    rewrap(1)
-    for a, b in BANKS:
-        mm(R("PC", a, b), [(R("ID"), R("BB", 3 * V + a, 3 * V + b)), (R("NI"), R("c1w", a, b))], True, False)
+    got = [0, 0]
+
+    def invert(q, s, n):
+        a = got[s]
+        n = min(n, KV - a)
+        got[s] += n
+        o = IX(R("WW", INV[s], INV[s] + U), lst("pl", s * 192 + a // 16, n // 16))
+        if q == "s":
+            act(o, R("BA", a, a + n), F.Silu)
+        else:
+            cp(o, R("BA", a, a + n))
+        if got[s] == KV:
+            dma("y", [(R("ld", (s + 1) * LD + 8, (s + 2) * LD), few(s))])
+
+    clear = [n * U + u * W for n in GZERO for u in range(4)]
+
+    def sweep(n):
+        for a in clear[:n]:
+            iota(R("WW", a, a + W), [[0, W]], 0, 0)
+        del clear[:n]
+
+    two = ((0, 192), (192, 416))
+    for a, b in two:
+        ts(R("fui", a, b), R("fui", 1152 + a, 1152 + b), 4, A.arith_shift_right)
+    for a, b in two:
+        ts(P(PT + a, PT + b), R("fui", a, b), -4095.0 / 256.0, A.mult)
+    for a, b in two:
+        tt(P(PT + a, PT + b), R("fui", 1152 + a, 1152 + b), P(PT + a, PT + b), A.add)
+    for a, b in two:
+        ts(R("pl", a, b), P(PT + a, PT + b), 256.0, A.mult)
+    invert("s", 0, SA)
+    dma("y", [(R("fui", 0, V), (T.fu[:, 0:V], [], []))])
+    cp(R("A1", 0, V), R("cli"))
+    cp(R("sm", 0, 8), R("cri"))
+    ts(R("cli", 384, V), R("fui", V, 1152), W - 1, A.bitwise_and)
+    cp(R("sm", 8, 10), R("thi", 0, 2))
+    ts(R("cli", 0, 384), R("fui", 1152, 2 * V), W - 1, A.bitwise_and)
+    cp(R("cc", 0, 384), R("cli", 384, V))
+    ts(R("sm", 11, 13), R("thi", 0, 2), -1.0, A.mult, 0.5, A.add)
+    invert("v", 1, VA)
+
+    def pack(which, PT=PT):
+        for mh in which:
+            ts(P(PT + mh % 2 * 192, PT + (mh % 2 + 1) * 192), R("fui", mh * 384, mh * 384 + 192), 4096.0, A.mult, 1.0, A.add)
+        for mh in which:
+            for k in range(4):
+                a = PT + mh % 2 * 192 + k * 48
+                tt(R("A2", mh * 192 + 3 - k, (mh + 1) * 192, 4), P(a, a + 48), lst("fui", mh * 384 + 192 + k * 48), A.add, apart=True)
+
+    pack(PKS[0])
+    dma("y", [(R("fui", V, 2 * V), (T.fu[:, V:2 * V], [], [])), (R("flw", 0, V), H("fl"))], after=[x0])
+    zero(ZERO[0], x0)
+
+    def join(at, parts, out, f, n=V, o=0):
+        for j, (name, c) in enumerate(parts):
+            for a, b in ((0, n // 2), (n // 2, n)) if n >= JS else ((0, n),):
+                dst = R(out, o + a, o + b) if out and j == len(parts) - 1 else P(at + a, at + b)
+                tt(dst, P(at + a, at + b), R(name, c + a, c + b), f)
+
+    steps = [(0, HALF), (HALF, V)] * bool(HALF) + [(k * V, (k + 1) * V) for k in range(1 if HALF else 0, 4)]
+    for a, b in steps:
+        act(R("BB", a, b), IX(R("A1"), lst("cc", a // 16, (b - a) // 16)), F.Identity, bias=col("sm", a // V))
+    for a, b in steps:
+        tt(R("BB", a, b), IX(R("A1"), lst("cc", 192 + a // 16, (b - a) // 16)), R("BB", a, b), A.add)
+    pe(PD, V, [("ID", "BB", 0)])
+    join(PD, [("BB", k * V) for k in (1, 2, 3)], "c1w", A.max)
+    cp(R("cc", 384, V), R("cli", 0, 384))
+    cp(R("sa"), IX(R("c1w", 0, V), lst("sndu", 16, 16)))
+    x1 = exchange(2, -1, ("sa", 0), ("c1w", V))
+    pe(PM, V, [("ID", "c1w", 0)])
+    sweep(GZ[0])
+
+    for x in INVC:
+        if x == "snd":
+            act(IX(R("WW", INV[2], INV[2] + U), lst("pl", 384, 32)), R("BA", 0, 4 * G), F.Silu)
+            dma("y", [(R("A2", 512, V), few(2))])
+        elif x == "pack":
+            pack(PKS[1])
+        elif x == "c1t":
+            act(R("A3"), R("c1w", 0, V), F.Identity, bias=col("sm", 8))
+        elif x == "sf":
+            act(R("sf"), IX(R("flw", 0, V), lst("sndu", 0, 16)), F.Copy)
+            exchange(1, -1, ("sf", 0), ("flw", V))
+            sweep(GZ[1])
+        else:
+            invert(*x)
+    zero(ZERO[1], x1)
+    XC = KV - 512 * XB
+    pe(PD, 5 * 512, [("NI", "BB", 0)], True, False)
+    l = R("ID" if XB else "NI")
+    mm(P(5 * 512, KV), [(l, R("BB", 5 * 512, KV))] + ([(R("NI"), R("c1w", 256, V))] if XB else []), True, False)
+
+    for a, b in steps:
+        act(R("BC", 64 + a, 64 + b), IX(R("c1w"), lst("cc", 384 + a // 16, (b - a) // 16)), F.Identity, bias=col("sm", 4 + a // V))
+    for n in range(2):
+        ts(R("inv", 512 + n * G, 640 + n * G), R("A2", 512 + n * G, 640 + n * G), -55.75 - n * 2 * G, A.add)
+    for a, b in steps:
+        tt(R("BC", 64 + a, 64 + b), IX(R("c1w"), lst("cc", 576 + a // 16, (b - a) // 16)), R("BC", 64 + a, 64 + b), A.add)
+        if b == 2 * V:
+            ts(R("inv", 256, 512), R("ld", 2 * LD + 8, 3 * LD), 0.25, A.add)
+        if b == LATEC * V:
+            ts(R("inv", 0, 256), R("ld", LD + 8, 2 * LD), 0.25, A.add)
+    if "c1t" not in INVC:
+        act(R("A3"), R("c1w", 0, V), F.Identity, bias=col("sm", 8))
+    if "sf" not in INVC:
+        act(R("sf"), IX(R("flw", 0, V), lst("sndu", 0, 16)), F.Copy)
+        exchange(1, -1, ("sf", 0), ("flw", V))
+        sweep(GZ[1])
+    cuts = sorted(set(list(range(0, XC + 1, 512)) + list(range(0, XC, V))))
+    for a, b in zip(cuts, cuts[1:]):
+        mm(P(a, b), [(R("ID"), R("A3", a % V, a % V + b - a))], False, b % 512 == 0)
+
+    def uses(y, n, c, room, at):
+        bufs = room[:8 - y]
+        for j, (name, a) in enumerate(bufs):
+            act(R(name, a, a + n), IX(R("BC"), lst("inv", j * 64 + c // 16, n // 16)), F.Copy)
+        for j in range(8 - y):
+            if j < y:
+                name, a = bufs[j]
+                tt(R(name, a, a + n), IX(R("BC"), lst("inv", (7 - j) * 64 + c // 16, n // 16)), R(name, a, a + n), A.max)
+            if j:
+                join(at, bufs[j - 1:j], None, A.max, n)
+        return bufs[-1]
+
+    def home(level, land, at, x, y, out, f):
+        win = R("ld", land * LD, (land + 1) * LD)
+        if HS[land]:
+            for d in (0, 1):
+                for a, b in SIDES:
+                    act(R(y[0], y[1] + d * V + a, y[1] + d * V + b), IX(win, lst("inv", 512 + d * 64 + level * 128 + a // 16, 24)), F.Copy)
+            join(at, [x, y, (y[0], y[1] + V)], out, f)
+            return
+        for a, b in SIDES:
+            act(R(y[0], y[1] + a, y[1] + b), IX(win, lst("inv", 576 + level * 128 + a // 16, 24)), F.Copy)
+        for a, b in SIDES:
+            part = R(x[0], x[1] + a, x[1] + b)
+            tt(part, IX(win, lst("inv", 512 + level * 128 + a // 16, 24)), part, f)
+        join(at, [x, y], out, f)
+
+    bufs = [R("BE", 2 * V + j * 256, 2 * V + (j + 1) * 256) for j in range(5)]
+    cp(bufs[4], IX(R("BC"), lst("inv", 7 * 64 + 48, 16)))
+    for j in range(4):
+        act(bufs[j], IX(R("BC"), lst("inv", j * 64 + 48, 16)), F.Copy)
+    for j in range(3):
+        tt(bufs[j], IX(R("BC"), lst("inv", (6 - j) * 64 + 48, 16)), bufs[j], A.max)
+        if j == 1:
+            tt(P(PM + V, PM + W), bufs[4], bufs[0], A.max)
+    join(PM + V, [("BE", 2 * V + j * 256) for j in (1, 3, 2)], "A1", A.max, 2 * G, V)
+    x2 = exchange(3, 1, ("A1", V), ("ld", 8))
+    kept = uses(YO, V, 0, [("BA", j * V) for j in range(4)] + [("BE", j * V) for j in range(2)], PM)
+    sweep(99)
+    zero(ZERO[2], x2)
+
+    home(1, 0, PM, kept, ("BA", 0), "A1", A.max)
+    pack(PKS[2], 3584)
 
     def votes(m, k):
-        mm(R("PV%d" % m, 3 - k, 192, 4),
-           [(R("E", 15 - i, 143 - i), R("VB", k * V + i, (k + 1) * V, 16)) for i in range(16)])
+        a = m * KV + k * V
+        mm(P(PV[m] + 3 - k, PV[m] + 192, 4), [(R("E", 15 - i, 143 - i), R("VB", a + i, a + V, 16)) for i in range(16)])
 
+    PV = (0, KV)
     for k in range(4):
-        act(piece("VB", k), piece("BC", k, 64), F.Sign, bias=col("sm", 12))
-        votes(1, k)
-    act(R("PA", 0, V), R("c1w", 0, V), F.Identity, bias=col("sm", 8))
-
-    ts(R("inv", 0, 256), R("ld", 256, 512), 0.25, A.add)
-    for mh in range(PK1, 4):
-        pack(mh, 0)
-    for u in range(4):
-        for a in (0, 512):
-            tt(R("A1", a, a + 512), IX(R("BC"), lst("inv", u * 64 + a // 16, 32)), R("A1" if u else "c1w", a, a + 512), A.max)
-    for mh in range(PK1, PK2):
-        pack(mh, 1)
-    ts(R("inv", 256, 512), R("ld", 512, 768), 0.25, A.add)
-    for u in range(4):
-        for a in (0, G):
-            tt(R("A1", V + a, V + a + G), IX(R("BC"), lst("inv", 256 + u * 64 + 48 + a // 16, 8)), R("A1", V + a, V + a + G), A.max)
-    x2 = exchange(3, 1, ("A1", V), ("ld", 0))
-    for u in range(4):
-        for a, b in SIDES:
-            tt(R("A1", a, b), IX(R("BC"), lst("inv", 256 + u * 64 + a // 16, 24)), R("A1", a, b), A.max)
-    for mh in range(PK2, 4):
-        pack(mh, 1)
-    for n in range(3):
-        dma("y", [(R("W%d" % n, 0, 4 * W), R("W3", 0, 4 * W))], after=[x2])
+        act(piece("VB", k, KV), piece("BC", k, 64), F.Sign, bias=col("sm", 12))
     act(R("A3"), R("topb"), F.Copy, scale=BIG)
-    for q in range(4):
+    if XB:
+        mm(P(XC, KV), [(R("ID"), R("A1", 256, V))], False, True)
+        act(R("VB", XC, KV), P(XC, KV), F.Sign, bias=col("sm", 11))
+    for q in (0, 2, 1, 3):
         act(piece("BE", q), R("A3"), F.Copy, scale=col("fwf", 4 + q))
-    act(R("W4", 0, 2 * W), R("W3", 0, 2 * W), F.Copy)
-
-    def merge(name, level, land, f):
-        acc = R(name, 0, V)
-        l1, l2 = lst("sndu", level * 16, 8), lst("sndu", level * 16 + 8, 8)
-        cp(R("tm", 0, G), IX(acc, l1))
-        tt(IX(acc, l1), R("tm", 0, G), R("ld", land, land + G), f)
-        tt(R("tm", G, 2 * G), IX(acc, l2), R("ld", land + G, land + 2 * G), f)
-        cp(IX(acc, l2), R("tm", G, 2 * G))
-
-    merge("A1", 1, 0, A.max)
-
-    for a, b in BANKS:
-        mm(R("PC", a, b), [(R("ID"), R("A1", a, b))], False, True)
-    act(piece("VB", 3), R("PC", 0, V), F.Sign, bias=col("sm", 11))
-    if SMASK:
-        act(R("tm", 0, 192), R("PV1", 0, 192), F.Sign, bias=1.0)
-        act(R("PV1", 192, 384), R("tm", 0, 192), F.Relu)
-        act(R("PV1", 0, 192), R("tm", 0, 192), F.Relu)
-        act(R("tm", 0, 192), R("tm", 0, 192), F.Relu, scale=-1.0)
-        act(R("PV1", 0, 192, 4), R("PV1", 0, 192, 4), F.Copy, scale=0.0)
-        act(R("tm", 0, 192, 4), R("tm", 0, 192, 4), F.Copy, scale=0.0)
-    act(R("PB", 0, V), R("topb"), F.Copy, scale=BIG)
-    act(R("W4", 2 * W, 4 * W), R("W3", 2 * W, 4 * W), F.Copy)
-    iota(R("W5", 0, 2 * W), [[0, 2 * W]], 0, 0)
-    for a, b in SIDES:
-        tt(R("PA", a, b), R("PA", a, b), R("A1", a, b), A.subtract)
-    for k in range(3):
-        for a, b in SIDES if k == 0 else ((0, V),):
-            tt(R("VB", k * V + a, k * V + b), R("BB", k * V + a, k * V + b), R("PA", a, b), A.is_ge)
+    for k in range(4):
+        b = min((k + 1) * V, XC)
+        tt(R("VB", k * V, b), P(k * V, b), R("A1", 0, b - k * V), A.is_le)
         votes(0, k)
-        if k == 1:
-            votes(0, 3)
+    pack(PKS[3], 3584)
 
-    def choose(m):
-        pv = "PV%d" % m
-        pi = R("fui", 576 * m, 576 * m + 192)
-        dead, later = R("BC", 1536, 1728), R("PC", V, V + 192)
+    TB = KV - 1728
+
+    def choose(m, early):
+        pv, pi = PV[m], 576 * m
+        live = P(pv + 192, pv + 384)
         if m == 0:
-            tt(R(pv, 192, 384), R(pv, 0, 192), R("CC", V, V + 192), A.is_ge)
-        elif not SMASK:
-            ts(R(pv, 192, 384), R(pv, 0, 192), 0.0, A.is_ge)
-        if m == 1 and SMASK:
-            dead, later = R("tm", 0, 192), R(pv, 0, 192)
+            dead, later = R("BB", TB + 1536, TB + 1728), P(512, 704)
+            tt(live, P(pv, pv + 192), R("CC", 384, 576), A.is_ge)
+            tt(dead, P(pv, pv + 192), R("CC", 0, 192), A.is_lt)
         else:
-            tt(dead, R(pv, 0, 192), R("CC", m * 384, m * 384 + 192), A.is_lt)
+            dead, later = R("tm", 0, 192), P(pv, pv + 192)
+
+        def unpack(a, b):
+            ts(R("fui", pi + a, pi + b), R("BB", TB + 387 + 4 * a, TB + 384 + 4 * b, 4), -1.0, A.add)
+
+        def child(s, a, b):
+            x = R("fui", 192 + s * 192 + a, 192 + s * 192 + b)
+            if s == 0:
+                ts(x, R("fui", pi + a, pi + b), 12, A.arith_shift_right, 0x13FF, A.bitwise_and)
+            else:
+                ts(x, R("fui", pi + a, pi + b), 2 ** 24 + W - 1, A.bitwise_and)
+            ts(R("fc", m * 384 + s * 192 + a, m * 384 + s * 192 + b), x, float(W), A.min)
+
+        def spare():
+            mm(P(pv, pv + 192), [(R("ID"), R("DU")), (R("N8"), R("BB", TB + 387, TB + 1152, 4))])
+
+        def second():
+            for h in range(2):
+                tt(R("BB", TB + 1152 + h * 192, TB + 1344 + h * 192), later, R("BB", TB + 383 + h * 192, TB + 575 + h * 192), A.mult)
+            for h in range(2):
+                scan(R("BB", TB + 768 + h * 192, TB + 960 + h * 192), dead, R("BB", TB + 1152 + h * 192, TB + 1344 + h * 192))
+
         for h in range(2):
             a = (m * 2 + h) * 192
-            tt(R("BC", h * 192, (h + 1) * 192), R(pv, 192, 384), R("A2", a, a + 192), A.mult)
-        if m == 0 or not SMASK:
-            tt(later, R(pv, 0, 192), R("CC", m * 384 + 192, (m + 1) * 384), A.is_ge)
+            tt(R("BB", TB + h * 192, TB + (h + 1) * 192), live, R("A2", a, a + 192), A.mult)
         for h in range(2):
-            scan(R("BC", 384 + h * 192, 576 + h * 192), dead, R("BC", h * 192, (h + 1) * 192))
-        for h in range(2):
-            tt(R("BC", 1152 + h * 192, 1344 + h * 192), later, R("BC", 383 + h * 192, 575 + h * 192), A.mult)
-        for h in range(2):
-            scan(R("BC", 768 + h * 192, 960 + h * 192), dead, R("BC", 1152 + h * 192, 1344 + h * 192))
-        ts(pi, R("BC", 387, 1152, 4), -1.0, A.add)
-        mm(R(pv, 0, 192), [(R("ID"), R("DU")), (R("N8"), R("BC", 387, 1152, 4))])
-        ts(R("fui", 192, 384), pi, 12, A.arith_shift_right, 0x13FF, A.bitwise_and)
-        ts(R("fui", 384, 576), pi, W - 1, A.bitwise_and)
-        ts(R("fc", m * 384, (m + 1) * 384), R("fui", 192, 576), float(W), A.min)
+            scan(R("BB", TB + 384 + h * 192, TB + 576 + h * 192), dead, R("BB", TB + h * 192, TB + (h + 1) * 192))
+        if m == 0:
+            tt(later, P(pv, pv + 192), R("CC", 192, 384), A.is_ge)
+        if early:
+            weave(weave(hold(unpack, 0, 96) + hold(child, 0, 0, 96), hold(second)), [])
+            rest = weave([LAT] + hold(unpack, 96, 192) + hold(child, 0, 96, 192) + hold(child, 1, 96, 192),
+                         hold(child, 1, 0, 96) + hold(place, m, 0, 96) + hold(place, m, 96, 192))
+            spare()
+            return rest
+        second()
+        unpack(0, 192)
+        spare()
+        left, right = hold(child, 0, 0, 192), hold(child, 1, 0, 192)
+        held[-1].extend([left[0], right[0], left[1], right[1]])
 
-    def places(m):
-        pi = R("fui", 576 * m, 576 * m + 192)
-        spare = R("PV%d" % m, 0, 192)
-        ts(R("cli", 0, 192), pi, 12, A.arith_shift_right)
-        ts(R("cli", 192, 384), pi, 4 * W - 1, A.bitwise_and)
+    def place(m, a, b):
+        pi = R("fui", 576 * m + a, 576 * m + b)
+        ts(R("cli", a, b), pi, 12, A.arith_shift_right)
+        ts(R("cli", 192 + a, 192 + b), pi, U - 1, A.bitwise_and)
+
+    def strip(m):
         for s in range(2):
-            tt(R("cli", 384 + s * 192, 576 + s * 192), R("cli", s * 192, (s + 1) * 192), spare, A.max)
-        cp(R("fz", m * 384, (m + 1) * 384), R("cli", 384, V))
+            tt(R("cli", 384 + s * 192, 576 + s * 192), R("cli", s * 192, (s + 1) * 192), P(PV[m], PV[m] + 192), A.max)
+        for s in range(2):
+            cp(R("fz", m * 384 + s * 192, m * 384 + (s + 1) * 192), R("cli", 384 + s * 192, 576 + s * 192))
 
-    choose(0)
+    for k in range(V1):
+        votes(1, k)
+    rest = choose(0, True)
 
     for q in range(4):
         act(piece("BA", q), IX(R("flw"), lst("fc", q * 48)), F.Copy, scale=col("fwf", q))
-    places(0)
     for q in range(4):
-        tt(piece("BC", q, 64), IX(R("flw"), lst("fc", 192 + q * 48)), piece("BA", q), A.mult)
+        tt(piece("BB", q), IX(R("flw"), lst("fc", 192 + q * 48)), piece("BA", q), A.mult)
         if q < PE_SUM:
-            for a, b in ((0, 512), (512, V)):
-                mm(R("PA", a, b), [(R("ID"), R("BC", 64 + q * V + a, 64 + q * V + b))], q == 0, q == PE_SUM - 1)
-        if q == 0 and not PE_SUM:
-            act(R("PA", 0, V), piece("BC", 0, 64), F.Copy)
-    join("BC", 64, "i1w", A.add, max(PE_SUM, 1))
+            pe(W, V, [("ID", "BB", q * V)], q == 0, q == PE_SUM - 1)
+    for k in range(V1, 4):
+        votes(1, k)
+    join(W, [("BB", q * V) for q in range(PE_SUM, 4)], "i1w", A.add)
+    rest = weave([LAT], rest + hold(strip, 0))
     cp(R("sa"), IX(R("i1w", 0, V), lst("sndu", 16, 16)))
-    exchange(4, -1, ("sa", 0), ("i1w", V))
-    for q in range(4):
-        act(piece("BD", q), IX(R("flw"), lst("fc", 192 + q * 48)), F.Copy, scale=col("fwf", q))
-    act(R("W5", 2 * W, 4 * W), R("W3", 2 * W, 4 * W), F.Copy)
-    choose(1)
-    places(1)
+    x4 = exchange(4, -1, ("sa", 0), ("i1w", V))
+    zero(ZERO[3], x4)
+    for q in (0, 2, 1, 3)[:BDE]:
+        act(piece("BC", q), IX(R("flw"), lst("fc", 192 + q * 48)), F.Copy, scale=col("fwf", q))
+    pv = PV[1]
+    act(R("tm", 0, 192), P(pv, pv + 192), F.Sign, bias=1.0)
+    act(P(pv + 192, pv + 384), R("tm", 0, 192), F.Relu)
+    act(P(pv, pv + 192), R("tm", 0, 192), F.Relu)
+    act(R("tm", 0, 192), R("tm", 0, 192), F.Relu, scale=-1.0)
+    act(P(pv, pv + 192, 4), P(pv, pv + 192, 4), F.Copy, scale=0.0)
+    act(R("tm", 0, 192, 4), R("tm", 0, 192, 4), F.Copy, scale=0.0)
+    for q in (0, 2, 1, 3)[BDE:]:
+        act(piece("BC", q), IX(R("flw"), lst("fc", 192 + q * 48)), F.Copy, scale=col("fwf", q))
+    weave(weave(hold(choose, 1, False), rest), [])
+    place(1, 0, 192)
+    strip(1)
 
-    def target(win, m, s, q):
-        return IX(R(win), lst("fz", m * 384 + s * 192 + q * 48))
+    PO, PA, PG, PB, PY = 0, V, 1536, 2048, 3072
+    oP = P(PO, PO + V)
 
-    def product(name, q, o):
-        tt(piece(name, q), piece(name, q), o, A.mult)
+    def target(n, m, s, q):
+        return IX(R("WW", n * U, (n + 1) * U + STRIP), lst("fz", m * 384 + s * 192 + q * 48))
 
-    def halve(win):
-        if FOLD2:
-            dma("g", [(R(win, u * W, u * W + V), R(win, (u + 2) * W, (u + 2) * W + V)) for u in range(2)], accum_op=A.add)
+    def part(n, m, a, b):
+        return IX(R("WW", n * U, (n + 1) * U + STRIP), lst("fz", m * 384 + 336 + a // 16, (b - a) // 16))
+
+    def ghosts(n, first, us=(0, 1, 2, 3), last=False):
+        mm(P(PG, PG + 2 * G), [(R("ID"), R("WW", n * U + u * W + V, n * U + (u + 1) * W)) for u in us], first, last)
+
+    def halve(a, b):
+        if ONE:
+            dma("g", [(R("WW", a, a + W + V), R("WW", b, b + W + V))], accum_op=A.add)
         else:
-            dma("g", [(R(win, 0, W + V), R(win, 2 * W, 3 * W + V))], accum_op=A.add)
+            dma("g", [(R("WW", a + u * W, a + u * W + V), R("WW", b + u * W, b + u * W + V)) for u in range(2)], accum_op=A.add)
 
-    PG = R("PV0", 0, 2 * G)
-
-    def ghosts_pe(win, first, last):
-        mm(PG, [(R("ID"), R(win, u * W + V, (u + 1) * W)) for u in range(4)], first, last)
-
-    def last_ghosts(win, out, scale=None):
-        if not VGH:
-            ghosts_pe(win, False, True)
-            act(R(out), PG, F.Copy, scale=scale or 1.0)
-            return
-        mm(PG, [(R("ID"), R(win, u * W + V, (u + 1) * W)) for u in range(2)], False, True)
-        tt(R("tm"), R(win, 2 * W + V, 3 * W), R(win, 3 * W + V, 4 * W), A.add)
-        if scale is None:
-            tt(R(out), PG, R("tm"), A.add)
+    def done(n, first, last=False, how="raw"):
+        if how == "half":
+            dma("g", [(R("WW", n * U, n * U + 2 * W), R("WW", n * U + 2 * W, (n + 1) * U))], accum_op=A.add)
+            ghosts(n, first, (0, 1), last)
+        elif how == "v":
+            halve(n * U, n * U + 2 * W)
+        elif ONE:
+            ghosts(n, first, (0,))
+            halve(n * U, n * U + 2 * W)
+            ghosts(n, False, (1, 2, 3), last)
         else:
-            for a in (0, G):
-                tt(R("PV0", a, a + G), R("PV0", a, a + G), R("tm", a, a + G), A.add)
-            for a in (0, G):
-                ts(R(out, a, a + G), R("PV0", a, a + G), scale, A.mult)
+            ghosts(n, first, last=last)
+            halve(n * U, n * U + 2 * W)
 
-    def add_own(slices, out, first, sides=SIDES):
-        todo = list(slices)
-        if first:
-            (w0, u0), (w1, u1) = todo.pop(0), todo.pop(0)
-            for a, b in sides:
-                tt(R("PA", a, b), R(w0, u0 * W + a, u0 * W + b), R(w1, u1 * W + a, u1 * W + b), A.add)
-        for n, (w, u) in enumerate(todo):
-            for a, b in sides:
-                tt(R(out if out and n == len(todo) - 1 else "PA", a, b), R("PA", a, b), R(w, u * W + a, u * W + b), A.add)
+    def pair(x, y):
+        for a, b in SIDES:
+            tt(P(PA + a, PA + b), R("WW", x[1] + a, x[1] + b), R("WW", y[1] + a, y[1] + b), A.add)
 
-    def halves(w):
-        return [(w, 0), (w, 1)]
+    def finish(wins, plan, last, fill_in, ahead, out, n, land, scale, res):
+        wa, wb, wc, wd = wins
+        vpre, pre, post, share, two, how = plan
+        halves = [("WW", w * U + u * W) for w in ((wa, wc) if two else (wa, wb, wc)) for u in (0, 1)]
+        mine, halves = halves[:vpre], halves[vpre:]
+        if two == 1:
+            halve(wa * U, wb * U)
+        for j in range(pre):
+            pe(PB, V, [("ID",) + halves[j]], j == 0, j == pre + post - 1)
+        done(wc, False, DG != "p", how)
+        if two == 2:
+            halve(wa * U, wb * U)
+        last()
+        if DG == "p":
+            ghosts(wd, False, last=True)
+        for j in range(pre, pre + post):
+            pe(PB, V, [("ID",) + halves[j]], j == 0, j == pre + post - 1)
+        fill_in()
+        if how == "v":
+            join(PG, [("WW", wc * U + u * W + V) for u in range(4)], None, A.add, 2 * G)
+        if mine:
+            pair(*mine[:2])
+            join(PA, mine[2:], None, A.add)
+        gs = [R("WW", wd * U + u * W + V, wd * U + (u + 1) * W) for u in range(4)]
+        if DG == "v":
+            join(PG, [("WW", wd * U + u * W + V) for u in range(4)], None if scale else out, A.add, 2 * G)
+        if DG == "w":
+            tt(gs[0], gs[0], gs[1], A.add)
+            tt(gs[2], gs[2], gs[3], A.add)
+            join(PG, [("WW", wd * U + u * W + V) for u in (0, 2)], None if scale else out, A.add, 2 * G)
+        if scale or DG == "p":
+            act(R(out), P(PG, PG + 2 * G), F.Copy, scale=scale or 1.0)
+        exchange(n, 1, (out, 0), ("ld", land * LD + 8))
+        ahead()
+        todo = [("WW", wd * U + u * W) for u in range(4)] + halves[pre + post:]
+        kept = todo.pop()
+        if not mine:
+            pair(*todo[:2])
+            todo = todo[2:]
+        if not pre + post:
+            join(PA, todo, None, A.add)
+            return PA, kept
+        join(PA, todo, "A1", A.add)
+        join(PB, [("A1", 0)], None, A.add)
+        return PB, kept
 
-    def whole(w):
-        return [(w, u) for u in range(4)]
-
-    oS, oP = R("A3"), R("PB", 0, V)
+    oS = R("A3")
+    pe(PO, V, [("ID", "A3", 0)])
 
     def edge(q):
-        tt(piece("BC", q, 64), IX(R("i1w"), lst("fc", 576 + q * 48)), piece("BB", q), A.mult)
+        tt(piece("BB", q), IX(R("i1w"), lst("fc", 576 + q * 48)), piece("BB", q), A.mult)
 
-    for q in (0, 2, 1, 3):
-        if q not in LWV:
+    for h in (0, 1):
+        for q in (h, h + 2):
             act(piece("BB", q), IX(R("i1w"), lst("fc", 384 + q * 48)), F.Copy, scale=col("fwf", 4 + q))
-    for q in (0, 2, 1, 3):
-        tt(piece("BE", q), IX(R("i1w"), lst("fc", 576 + q * 48)), piece("BE", q), A.mult)
-    for q in LWV:
-        ts(piece("BB", q), IX(R("i1w"), lst("fc", 384 + q * 48)), col("fwf", 4 + q), A.mult)
-    for q in (0, 2):
-        act(target("W0", 1, 0, q), piece("BE", q), F.Silu)
-    ghosts_pe("W0", True, False)
-    halve("W0")
-    for q in (1, 3):
-        act(target("W2", 1, 0, q), piece("BE", q), F.Silu)
-    tt(target("W1", 1, 1, 0), oS, piece("BB", 0), A.mult)
-    tt(target("W1", 1, 1, 2), oS, piece("BB", 2), A.mult)
-    ghosts_pe("W1", False, False)
-    halve("W1")
-    ghosts_pe("W2", False, False)
-    halve("W2")
-    if NVH == 2:
-        edge(1)
-        product("BB", 1, oP)
-        edge(3)
-        product("BB", 3, oP)
-        act(target("W3", 1, 1, 1), piece("BB", 1), F.Silu)
-    else:
-        tt(target("W3", 1, 1, 1), oS, piece("BB", 1), A.mult)
-        if NVH == 4:
-            tt(target("W3", 1, 1, 3), oS, piece("BB", 3), A.mult)
-        edge(3)
-        if NVH == 3:
-            product("BB", 3, oP)
-    if NVH < 4:
-        act(target("W3", 1, 1, 3), piece("BB", 3), F.Silu)
-    order = (3, 1, 0, 2)
-    for q in order[NVH == 2 and 2 or 1:4 - LATE]:
-        edge(q)
-    add_own(halves("W0"), None, True)
-    last_ghosts("W3", "sb")
-    exchange(5, 1, ("sb", 0), ("ld", 256))
+        for q in (h, h + 2):
+            tt(piece("BE", q), IX(R("i1w"), lst("fc", 576 + q * 48)), piece("BE", q), A.mult)
+        for q in (h, h + 2):
+            act(target(4 * h, 1, 0, q), piece("BE", q), F.Silu)
+        if h == 0:
+            for q in (0, 2):
+                tt(target(2, 1, 1, q), oS, piece("BB", q), A.mult)
+            done(0, True, how=GH2[0])
+            done(2, False, PLAN2[5] == "v", GH2[1])
+    tt(target(6, 1, 1, 1), oS, piece("BB", 1), A.mult)
+    if CUT2 < V:
+        tt(R("BE", CUT2, V), R("BB", 3 * V + CUT2, 4 * V), P(PO + CUT2, PO + V), A.mult)
+    if CUT2:
+        tt(part(6, 1, 0, CUT2), R("A3", 0, CUT2), R("BB", 3 * V, 3 * V + CUT2), A.mult)
+    order = (0, 2, 1, 3)
 
-    def sum_edges(qs, first, last):
-        for a, b in BANKS:
-            mm(R("PC", a, b), [(R("ID"), R("BC", 64 + q * V + a, 64 + q * V + b)) for q in qs], first, last)
-        if last:
-            act(R("A2"), R("PC", 0, V), F.Copy)
-            dma("y", [(H("yi"), R("A2"))])
+    def edges(qs):
+        for q in qs:
+            edge(q)
 
-    act(R("W0", 2 * W, 4 * W), R("W4", 0, 2 * W), F.Copy)
-    iota(R("W1", 2 * W, 4 * W), [[0, 2 * W]], 0, 0)
-    parts = {"v": halves("W1"), "c": whole("W3"), "b": halves("W2")}
-    add_own([x for n in ORD_H for x in parts[n]], "A1", False)
-    for n in (0, 1):
-        act(R("W%d" % n, 0, 2 * W), R("W4", 0, 2 * W), F.Copy)
-    merge("A1", 1, 256, A.add)
+    def last():
+        if CUT2 < V:
+            act(part(6, 1, CUT2, V), R("BE", CUT2, V), F.Silu)
+        act(oP, piece("BC", 2), F.Copy)
+
+    EARLY = ((0, 256, PB + V), (256, V, PG))
+
+    def ahead():
+        for a, b, at in EARLY[::-1]:
+            act(P(at, at + b - a), R("BC", a, b), F.Copy)
+
+    at, kept = finish((0, 2, 4, 6), PLAN2, last, lambda: edges(order[:YIN]), ahead, "sa", 5, 1, None, "A1")
+
+    def gather_yi(qs):
+        for q in qs:
+            if YS == "p":
+                pe(PY, V, [("ID", "BB", q * V)], q == order[0], q == order[3])
+            elif q != order[0]:
+                dma("g", [(piece("BB", order[0]), piece("BB", q))], accum_op=A.add)
+
+    gather_yi(order[:YIN])
+    if YS != "p":
+        act(P(PY, PY + V), piece("BC", 3), F.Copy)
+    home(1, 1, at, kept, ("BE", V), "A1", A.add)
+    act(P(PA + CUT1, PA + V), R("BA", 3 * V + CUT1, 4 * V), F.Copy)
 
     oS = R("A1", 0, V)
-    act(oP, oS, F.Copy)
-    for a, b in SIDES:
-        tt(R("BD", a, b), R("BD", a, b), R("A1", a, b), A.mult)
-    product("BD", 2, oP)
-    sum_edges(order[:4 - LATE], True, not LATE)
-    for a, b in SIDES:
-        act(IX(R("W4"), lst("fz", a // 16, 24)), R("BD", a, b), F.Silu)
-    act(target("W4", 0, 0, 2), piece("BD", 2), F.Silu)
-    ghosts_pe("W4", True, False)
-    halve("W4")
-    tt(target("W5", 0, 1, 0), oS, piece("BA", 0), A.mult)
-    product("BD", 1, oP)
-    product("BD", 3, oP)
-    for q in (1, 3):
-        act(target("W0", 0, 0, q), piece("BD", q), F.Silu)
-    tt(target("W5", 0, 1, 2), oS, piece("BA", 2), A.mult)
-    ghosts_pe("W5", False, False)
-    halve("W5")
-    ghosts_pe("W0", False, False)
-    halve("W0")
-    cut = 3 * V + CUT
-    tt(R("BA", cut, 4 * V), R("BA", cut, 4 * V), R("PB", CUT, V), A.mult)
-    tt(target("W1", 0, 1, 1), oS, piece("BA", 1), A.mult)
-    if CUT:
-        tt(IX(R("W1"), lst("fz", 336, CUT // 16)), R("A1", 0, CUT), R("BA", 3 * V, cut), A.mult)
-    act(IX(R("W1"), lst("fz", 336 + CUT // 16, (V - CUT) // 16)), R("BA", cut, 4 * V), F.Silu)
-    for q in order[4 - LATE:]:
-        edge(q)
-    add_own(halves("W4"), None, True, BANKS[::-1])
-    last_ghosts("W1", "sa", 1.0 / BIG)
-    exchange(6, 1, ("sa", 0), ("ld", 512))
-    parts = {"v": halves("W5"), "c": whole("W1"), "b": halves("W0")}
-    add_own([x for n in ORD_I for x in parts[n]], None, False, BANKS[::-1])
-    act(R("A3", 512, V), R("PA", 512, V), F.Copy, scale=1.0 / BIG)
-    ts(R("A3", 0, 512), R("PA", 0, 512), 1.0 / BIG, A.mult)
-    if not LATE_FIRST:
-        for q in order[4 - LATE:]:
-            edge(q)
-    if LATE:
-        sum_edges(order[4 - LATE:], False, True)
-    merge("A3", 0, 512, A.add)
+
+    def product(name, q, at, a=0):
+        x = R(name, q * V + a, (q + 1) * V)
+        if OP == "pre":
+            tt(x, P(at + a, at + V), R("A1", a, V), A.mult)
+        else:
+            tt(x, x, P(PO + a, PO + V), A.mult)
+
+    for a, b, at in EARLY:
+        tt(R("BC", a, b), P(at, at + b - a), R("A1", a, b), A.mult)
+    pe(PB, V, [("ID", "BC", V)])
+    tt(piece("BC", 2), oP, oS, A.mult)
+    if YS == "p":
+        pe(PO, V, [("ID", "BC", 3 * V) if OP == "pre" else ("ID", "A1", 0)])
+    for a, b, at in EARLY:
+        act(IX(R("WW", U, 2 * U + STRIP), lst("fz", a // 16, (b - a) // 16)), R("BC", a, b), F.Silu)
+    act(target(1, 0, 0, 2), piece("BC", 2), F.Silu)
+    done(1, True, how=GH1[0])
+    tt(target(3, 0, 1, 0), oS, piece("BA", 0), A.mult)
+    if CUT1 < V:
+        product("BA", 3, PA, CUT1)
+        act(part(7, 0, CUT1, V), R("BA", 3 * V + CUT1, 4 * V), F.Silu)
+    product("BC", 1, PB)
+    product("BC", 3, PO if YS == "p" else PY)
+    act(target(5, 0, 0, 1), piece("BC", 1), F.Silu)
+    tt(target(3, 0, 1, 2), oS, piece("BA", 2), A.mult)
+    done(3, False, PLAN1[5] == "v", GH1[1])
+    tt(target(7, 0, 1, 1), oS, piece("BA", 1), A.mult)
+    if CUT1:
+        tt(part(7, 0, 0, CUT1), R("A1", 0, CUT1), R("BA", 3 * V, 3 * V + CUT1), A.mult)
+    at, kept = finish((1, 3, 7, 5), PLAN1, lambda: act(target(5, 0, 0, 3), piece("BC", 3), F.Silu), lambda: edges(order[YIN:]),
+                      lambda: None, "sa", 6, 2, None, None)
+    gather_yi(order[YIN:])
+    if YS == "p":
+        act(R("A2"), P(PY, PY + V), F.Copy)
+    dma("y", [(H("yi"), R("A2") if YS == "p" else piece("BB", order[0]))])
+    home(0, 2, at, kept, ("BC", 0), None, A.add)
+    small = -at % 512 or 512
+    lo, hi = (0, small), (small, V)
+    for (a, b), q in zip((lo, hi), "sv" if small == 256 else "vs"):
+        if q == "s":
+            act(R("A3", a, b), P(at + a, at + b), F.Copy, scale=1.0 / BIG)
+        else:
+            ts(R("A3", a, b), P(at + a, at + b), 1.0 / BIG, A.mult)
     dma("y", [(H("yo"), R("A3"))])
 
     wait("g", list(count.items()))

from concourse.bass import DstId, RemoteDMATransfer
from concourse.mybir import AluOpType as A, ActivationFunctionType as F

V, W, G, KV = 768, 1024, 128, 3072
U = 4 * W
STRIP = V + G
LD = 8 + 2 * G
BIG = 2.0 ** 40
SIDES = ((0, V // 2), (V // 2, V))
f32, bf, i32, u16 = "float32", "bfloat16", "int32", "uint16"

SCRATCH = {}
for _n, _c, _t in [
    ("WW", 8 * U + STRIP, f32), ("BA", KV, f32), ("BB", KV, f32), ("BC", KV + 64, f32), ("BE", KV, f32),
    ("VB", 2 * KV, bf), ("A1", W, f32), ("c1w", W, f32), ("flw", W + 16, bf), ("i1w", W + 16, f32),
    ("A2", V, f32), ("A3", V, f32), ("sa", 256, f32), ("sf", 256, bf),
    ("ld", 3 * LD, f32), ("tm", 192, f32), ("cli", V, i32), ("fui", 2 * V + 32, i32), ("blk", 32, i32),
    ("sndi", 32, i32), ("cri", 8, i32), ("thi", 8, i32), ("fwf", 8, f32), ("sm", 16, f32), ("topb", V, bf),
    ("cc", V, u16), ("pl", 416, u16), ("inv", 768, u16), ("fc", V, u16), ("fz", V, u16), ("sndu", 32, u16),
    ("CC", 576, bf), ("DU", 192, f32), ("E", 144, bf), ("ID", 128, f32), ("NI", 128, f32), ("N8", 128, f32),
]:
    SCRATCH[_n] = ("sbuf", [128, _c], _t)
SCRATCH["PS"] = ("psum", [128, 4096], f32)

NDMA = 48
SEMAPHORES = ["v", "s", "p", "c"] + ["d%d" % _i for _i in range(NDMA)] + ["x%d" % _i for _i in range(7)] + ["l%d" % _i for _i in range(7)]
PR3 = True
YG, YO = 4, 2
XB = 0
PE_SUM = 2
YIN = 3
C1T = "late"
PLAN2 = (0, 1, 3, False, 0, "raw")
PLAN1 = (2, 0, 2, False, 0, "raw")
GH2 = ("raw", "raw")
GH1 = ("raw", "raw")
OP = "pre"
JS = 0
YS = "d"
BDE = 1
V1 = 4
ONE = False
HALF = 0
DG = "v"
ZERO = ((1,), (), (4, 5, 7), ())
GZERO = (2, 3, 6)
GZ = (4, 0)
SA, VA = 1280, 1152
PKS = ((), (0, 1), (), (2, 3))
LAT = 200
LATEC = 4
SKIPW = False
HS = (False, False, True)
INVC = (("s", 0, 256), "snd", ("s", 1, KV), ("v", 0, KV), "pack")
CUT2, CUT1 = 256, 128


def rank_program(g, core, T, topo):
    rank = T.rank_of(core)
    if rank is None:
        return
    N = len(T.cores)
    queue = {"v": g.vector, "s": g.scalar, "p": g.tensor, "g": g, "y": g.sync}
    own = {"v": "v", "s": "s", "p": "p", "g": "c"}
    count, waited, log, ndma = {}, {q: {} for q in queue}, {}, [0]

    def R(name, a=0, b=None, step=1):
        if b is None:
            b = T[name].shape[1]
        ap = T[name][:, a:b] if step == 1 else T[name][:, a:b:step]
        return (ap, [(name, a, b)], [])

    def IX(win, off):
        return (win[0].indirect(off[0]), win[1], off[1])

    def span(a, b):
        return a // 512 * 512, -(-b // 512) * 512

    def wait(q, tickets):
        need = {}
        for sem, val in tickets:
            need[sem] = max(need.get(sem, 0), val)
        for sem, val in need.items():
            if waited[q].get(sem, 0) < val:
                queue[q].wait_ge(T.sem[sem], val)
                waited[q][sem] = val

    def deps(q, reads, writes, compute):
        res = []
        for regs, isw in ((reads, False), (writes, True)):
            for name, a, b in regs:
                ps = SCRATCH[name][0] == "psum"
                for a2, b2, w2, q2, tk in log.get(name, []):
                    mine = compute and q2 == q
                    if ps and not mine:
                        lo, hi = span(a, b)
                        lo2, hi2 = span(a2, b2)
                        if lo < hi2 and lo2 < hi:
                            res.append(tk)
                    elif a < b2 and a2 < b and (w2 or isw):
                        if mine and isw and (q == "p" or (SKIPW and w2 and name == "WW")):
                            continue
                        res.append(tk)
        return res

    def note(q, reads, writes, tk):
        for regs, isw in ((reads, False), (writes, True)):
            for name, a, b in regs:
                log.setdefault(name, []).append((a, b, isw, q, tk))

    held = []

    def hold(f, *args):
        held.append([])
        f(*args)
        return held.pop()

    def weave(main, spare):
        now, past, spare = 0, [], list(spare)

        def touch(c):
            return [(r, True) for o in c[1] for r in o[1]] + [(r, False) for o in c[1] for r in o[2]] + \
                   [(r, False) for x in c[2] for r in x[1] + x[2]]

        def ready(c):
            return max([0] + [end + LAT for end, d in past for (n, a, b), w in touch(c) for (n2, a2, b2), w2 in touch(d)
                              if n == n2 and a < b2 and a2 < b and (w2 or w) and not (c[4] and w and w2)])

        def issue(c, start):
            op(*c)
            o = c[1][0]
            n = (o[2][0][2] - o[2][0][1]) * 40 if o[2] else max(64, o[0].shape[1])
            past.append((start + n, c))
            return start + n

        for c in main:
            if isinstance(c, int):
                until = now + c
            elif c[0] != "v":
                op(*c)
                continue
            else:
                until = ready(c)
            while spare and now + 32 < until and (spare[0][0] != "v" or ready(spare[0]) < until):
                if spare[0][0] != "v":
                    op(*spare.pop(0))
                else:
                    now = issue(spare[0], max(now, ready(spare[0])))
                    spare.pop(0)
            now = max(now, until) if isinstance(c, int) else issue(c, max(now, until))
        return spare

    def op(q, outs, ins, emit, apart=False):
        if held:
            held[-1].append((q, outs, ins, emit, apart))
            return
        writes = [r for o in outs for r in o[1]]
        reads = [r for o in outs for r in o[2]] + [r for x in ins for r in x[1] + x[2]]
        wait(q, deps(q, reads, [] if apart else writes, True))
        sem = own[q]
        count[sem] = count.get(sem, 0) + 1
        emit().then_inc(T.sem[sem], 1)
        note(q, reads, writes, (sem, count[sem]))

    def dma(q, pairs, after=(), **kw):
        sem = "d%d" % ndma[0]
        ndma[0] += 1
        writes = [r for o, x in pairs for r in o[1]]
        reads = [r for o, x in pairs for r in x[1]]
        wait(q, deps(q, reads, writes, False) + list(after))
        for o, x in pairs:
            queue[q].dma_start(o[0], x[0], **kw).then_inc(T.sem[sem], 16)
        count[sem] = 16 * len(pairs)
        note("dma", reads, writes, (sem, count[sem]))

    def H(name):
        return (T[name][:], [], [])

    def exchange(n, sign, src, dst):
        name, a = src
        name2, a2 = dst
        reads = [(name, a, a + 2 * G)]
        wait("g", deps("g", reads, [], False))
        trs, total = [], 0
        for d in (1, 2):
            peer = T.cores[(rank + sign * d) % N]
            eng = topo.engines(core, peer)
            half = len(eng) // 2
            mine = eng[:half] if d == 1 else eng[half:2 * half]
            rid, pid, _se = topo.addr(peer)
            trs.append(RemoteDMATransfer(dst_ids=[DstId(rid=rid, pnc=pid)], dma_engine_mask=sum(1 << e for e in mine),
                                         remote_sem=T.sem["x%d" % n], src=T[name][:, a + (d - 1) * G:a + d * G],
                                         dst=T[name2][:, a2 + (d - 1) * G:a2 + d * G]))
            total += len(mine)
        g.remote_dma_fused(trs, local_sem=T.sem["l%d" % n])
        count["l%d" % n] = total
        note("dma", reads, [], ("l%d" % n, total))
        come = sum(len(topo.engines(T.cores[(rank - sign * d) % N], core)) // 2 for d in (1, 2))
        count["x%d" % n] = come
        note("dma", [], [(name2, a2, a2 + 2 * G)], ("x%d" % n, come))
        return ("x%d" % n, come)

    def val(x):
        return x[0] if isinstance(x, tuple) else x

    def aps(*xs):
        return [x for x in xs if isinstance(x, tuple)]

    def cp(o, x):
        op("v", [o], [x], lambda: g.vector.tensor_copy(o[0], x[0]))

    def tt(o, x, y, f, apart=False):
        op("v", [o], [x, y], lambda: g.vector.tensor_tensor(o[0], x[0], y[0], f), apart)

    def ts(o, x, s1, f1, s2=None, f2=None):
        if f2 is None:
            op("v", [o], aps(x, s1), lambda: g.vector.tensor_scalar(o[0], x[0], val(s1), None, f1))
        else:
            op("v", [o], aps(x, s1, s2), lambda: g.vector.tensor_scalar(o[0], x[0], val(s1), val(s2), f1, f2))

    def scan(o, x, y):
        op("v", [o], [x, y], lambda: g.vector.tensor_tensor_scan(o[0], x[0], y[0], 0.0, A.mult, A.add))

    def fill(o, c):
        op("v", [o], [], lambda: g.vector.memset(o[0], c))

    def act(o, x, f, **kw):
        op("s", [o], aps(x, *kw.values()), lambda: g.scalar.activation(o[0], x[0], f, **{k: val(a) for k, a in kw.items()}))

    def iota(o, pat, base, cm):
        op("g", [o], [], lambda: g.iota(o[0], pat, base, cm, allow_small_or_imprecise_dtypes=True))

    def keep(o, pat, cmp, other, base, cm):
        op("g", [o], [o], lambda: g.affine_select(o[0], o[0], pat, cmp, other, base, cm))

    def mm(o, terms, first=True, last=True):
        def emit():
            ins = None
            for n, (l, r) in enumerate(terms):
                ins = g.tensor.matmul(o[0], l[0], r[0], first and n == 0, last and n == len(terms) - 1)
            return ins
        op("p", [o], [x for t in terms for x in t], emit)

    def pe(at, n, terms, first=True, last=True):
        a = at
        while a < at + n:
            b = min(at + n, a // 512 * 512 + 512)
            mm(P(a, b), [(R(l), R(name, c + a - at, c + b - at)) for l, name, c in terms], first, last)
            a = b

    def P(a, b, step=1):
        return R("PS", a, b, step)

    def piece(name, k, base=0):
        return R(name, base + k * V, base + (k + 1) * V)

    def lst(name, a, n=48):
        return R(name, a, a + n)

    def col(name, a):
        return R(name, a, a + 1)

    def zero(wins, after):
        for n in wins:
            dma("y", [(R("WW", n * U, (n + 1) * U), R("WW", 0, U))], after=[after])

    PD, PM, PT = 0, KV, 2560
    INV = (5 * U, 7 * U, 3 * U)

    def few(s):
        return (T.WW[0:128:18, INV[s]:INV[s] + U], [("WW", INV[s], INV[s] + U)], [])

    dma("y", [(R("sndi"), H("snd"))])
    dma("s", [(R("cli"), H("cl"))])
    dma("y", [(R("fui", V, 2 * V), H("cu"))])
    fill(R("WW", 0, 256), 0.0)
    fill(R("WW", 256, W), 0.0)
    fill(R("WW", W, 2 * W), 0.0)
    dma("y", [(few(0), R("WW", 0, 256))])
    dma("y", [(R("cri"), H("cr")), (R("thi", 0, 2), H("th")), (R("fwf"), H("fw"))])
    dma("y", [(few(s), R("WW", 0, 256)) for s in (2, 1)])
    fill(R("BC", 0, 64), 0.0)
    for n in range(3):
        fill(R("ld", n * LD, n * LD + 8), 0.0)
    iota(R("blk"), [[W, 4], [0, 8]], 0, 0)
    fill(R("flw", W, W + 16), 0.0)
    fill(R("i1w", W, W + 16), 0.0)
    for u in (2, 3):
        act(R("WW", u * W, (u + 1) * W), R("WW", 0, W), F.Silu)
    for k in (0, 1):
        iota(piece("BA", k), [[1, V]], 64 + k * V, 0)
    cp(R("sndu"), R("sndi"))
    tt(R("fui", 2 * V, 2 * V + 32), R("sndi"), R("blk"), A.add)
    cp(R("sa"), IX(R("cli"), lst("sndu", 0, 16)))
    x0 = exchange(0, -1, ("sa", 0), ("A1", V))
    iota(R("ID"), [[0, 128]], 1, 0)
    iota(R("NI"), [[0, 128]], -1, 0)
    keep(R("ID"), [[-1, 128]], A.is_equal, 0.0, 0, 1)
    keep(R("NI"), [[-1, 128]], A.is_equal, 0.0, 0, 1)
    for k in (2, 3):
        iota(piece("BA", k), [[1, V]], 64 + k * V, 0)
    dma("g", [(R("topb"), H("top"))])

    iota(R("E"), [[0, 144]], 1, 0)
    iota(R("CC", 0, 384), [[0, 384]], 8, 0)
    iota(R("CC", 384, 576), [[0, 192]], 8, 0)
    iota(R("N8"), [[0, 128]], -8192, 0)
    iota(R("DU"), [[0, 4], [16, 48]], U, 1)
    keep(R("E"), [[1, 144]], A.is_ge, 0.0, 0, -1)
    for n in range(2):
        keep(R("CC", n * 192, (n + 1) * 192), [[0, 48], [1, 4]], A.is_gt, 1e9 if n % 2 else -1e9, 0, 0)
    keep(R("E"), [[-1, 144]], A.is_ge, 0.0, 15, 1)
    keep(R("N8"), [[-1, 128]], A.is_equal, 0.0, 0, 1)
    if XB:
        keep(R("CC", 448, 576), [[0, 32], [1, 4]], A.is_gt, 0.0, 0, 0)
    keep(R("E"), [[0, 9], [1, 16]], A.is_ge, 0.0, -15, 0)

    got = [0, 0]

    def invert(q, s, n):
        a = got[s]
        n = min(n, KV - a)
        got[s] += n
        o = IX(R("WW", INV[s], INV[s] + U), lst("pl", s * 192 + a // 16, n // 16))
        if q == "s":
            act(o, R("BA", a, a + n), F.Silu)
        else:
            cp(o, R("BA", a, a + n))
        if got[s] == KV:
            dma("y", [(R("ld", (s + 1) * LD + 8, (s + 2) * LD), few(s))])

    clear = [n * U + u * W for n in GZERO for u in range(4)]

    def sweep(n):
        for a in clear[:n]:
            iota(R("WW", a, a + W), [[0, W]], 0, 0)
        del clear[:n]

    two = ((0, 192), (192, 416))
    for a, b in two:
        ts(R("fui", a, b), R("fui", 1152 + a, 1152 + b), 4, A.arith_shift_right)
    for a, b in two:
        ts(P(PT + a, PT + b), R("fui", a, b), -4095.0 / 256.0, A.mult)
    for a, b in two:
        tt(P(PT + a, PT + b), R("fui", 1152 + a, 1152 + b), P(PT + a, PT + b), A.add)
    for a, b in two:
        ts(R("pl", a, b), P(PT + a, PT + b), 256.0, A.mult)
    invert("s", 0, SA)
    dma("y", [(R("fui", 0, V), (T.fu[:, 0:V], [], []))])
    cp(R("A1", 0, V), R("cli"))
    cp(R("sm", 0, 8), R("cri"))
    ts(R("cli", 384, V), R("fui", V, 1152), W - 1, A.bitwise_and)
    cp(R("sm", 8, 10), R("thi", 0, 2))
    ts(R("cli", 0, 384), R("fui", 1152, 2 * V), W - 1, A.bitwise_and)
    cp(R("cc", 0, 384), R("cli", 384, V))
    ts(R("sm", 11, 13), R("thi", 0, 2), -1.0, A.mult, 0.5, A.add)
    invert("v", 1, VA)

    def pack(which, PT=PT):
        for mh in which:
            ts(P(PT + mh % 2 * 192, PT + (mh % 2 + 1) * 192), R("fui", mh * 384, mh * 384 + 192), 4096.0, A.mult, 1.0, A.add)
        for mh in which:
            for k in range(4):
                a = PT + mh % 2 * 192 + k * 48
                tt(R("A2", mh * 192 + 3 - k, (mh + 1) * 192, 4), P(a, a + 48), lst("fui", mh * 384 + 192 + k * 48), A.add, apart=True)

    pack(PKS[0])
    dma("y", [(R("fui", V, 2 * V), (T.fu[:, V:2 * V], [], [])), (R("flw", 0, V), H("fl"))], after=[x0])
    zero(ZERO[0], x0)

    def join(at, parts, out, f, n=V, o=0):
        for j, (name, c) in enumerate(parts):
            for a, b in ((0, n // 2), (n // 2, n)) if n >= JS else ((0, n),):
                dst = R(out, o + a, o + b) if out and j == len(parts) - 1 else P(at + a, at + b)
                tt(dst, P(at + a, at + b), R(name, c + a, c + b), f)

    steps = [(0, HALF), (HALF, V)] * bool(HALF) + [(k * V, (k + 1) * V) for k in range(1 if HALF else 0, 4)]
    for a, b in steps:
        act(R("BB", a, b), IX(R("A1"), lst("cc", a // 16, (b - a) // 16)), F.Identity, bias=col("sm", a // V))
    for a, b in steps:
        tt(R("BB", a, b), IX(R("A1"), lst("cc", 192 + a // 16, (b - a) // 16)), R("BB", a, b), A.add)
    pe(PD, V, [("ID", "BB", 0)])
    join(PD, [("BB", k * V) for k in (1, 2, 3)], "c1w", A.max)
    cp(R("cc", 384, V), R("cli", 0, 384))
    cp(R("sa"), IX(R("c1w", 0, V), lst("sndu", 16, 16)))
    x1 = exchange(2, -1, ("sa", 0), ("c1w", V))
    pe(PM, V, [("ID", "c1w", 0)])
    sweep(GZ[0])

    for x in INVC:
        if x == "snd":
            act(IX(R("WW", INV[2], INV[2] + U), lst("pl", 384, 32)), R("BA", 0, 4 * G), F.Silu)
            dma("y", [(R("A2", 512, V), few(2))])
        elif x == "pack":
            pack(PKS[1])
        elif x == "c1t":
            act(R("A3"), R("c1w", 0, V), F.Identity, bias=col("sm", 8))
        elif x == "sf":
            act(R("sf"), IX(R("flw", 0, V), lst("sndu", 0, 16)), F.Copy)
            exchange(1, -1, ("sf", 0), ("flw", V))
            sweep(GZ[1])
        else:
            invert(*x)
    zero(ZERO[1], x1)
    XC = KV - 512 * XB
    pe(PD, 5 * 512, [("NI", "BB", 0)], True, False)
    l = R("ID" if XB else "NI")
    mm(P(5 * 512, KV), [(l, R("BB", 5 * 512, KV))] + ([(R("NI"), R("c1w", 256, V))] if XB else []), True, False)

    for a, b in steps:
        act(R("BC", 64 + a, 64 + b), IX(R("c1w"), lst("cc", 384 + a // 16, (b - a) // 16)), F.Identity, bias=col("sm", 4 + a // V))
    for n in range(2):
        ts(R("inv", 512 + n * G, 640 + n * G), R("A2", 512 + n * G, 640 + n * G), -55.75 - n * 2 * G, A.add)
    for a, b in steps:
        tt(R("BC", 64 + a, 64 + b), IX(R("c1w"), lst("cc", 576 + a // 16, (b - a) // 16)), R("BC", 64 + a, 64 + b), A.add)
        if b == 2 * V:
            ts(R("inv", 256, 512), R("ld", 2 * LD + 8, 3 * LD), 0.25, A.add)
        if b == LATEC * V:
            ts(R("inv", 0, 256), R("ld", LD + 8, 2 * LD), 0.25, A.add)
    if "c1t" not in INVC:
        act(R("A3"), R("c1w", 0, V), F.Identity, bias=col("sm", 8))
    if "sf" not in INVC:
        act(R("sf"), IX(R("flw", 0, V), lst("sndu", 0, 16)), F.Copy)
        exchange(1, -1, ("sf", 0), ("flw", V))
        sweep(GZ[1])
    cuts = sorted(set(list(range(0, XC + 1, 512)) + list(range(0, XC, V))))
    for a, b in zip(cuts, cuts[1:]):
        mm(P(a, b), [(R("ID"), R("A3", a % V, a % V + b - a))], False, b % 512 == 0)

    def uses(y, n, c, room, at):
        bufs = room[:8 - y]
        for j, (name, a) in enumerate(bufs):
            act(R(name, a, a + n), IX(R("BC"), lst("inv", j * 64 + c // 16, n // 16)), F.Copy)
        for j in range(8 - y):
            if j < y:
                name, a = bufs[j]
                tt(R(name, a, a + n), IX(R("BC"), lst("inv", (7 - j) * 64 + c // 16, n // 16)), R(name, a, a + n), A.max)
            if j:
                join(at, bufs[j - 1:j], None, A.max, n)
        return bufs[-1]

    def home(level, land, at, x, y, out, f):
        win = R("ld", land * LD, (land + 1) * LD)
        if HS[land]:
            for d in (0, 1):
                for a, b in SIDES:
                    act(R(y[0], y[1] + d * V + a, y[1] + d * V + b), IX(win, lst("inv", 512 + d * 64 + level * 128 + a // 16, 24)), F.Copy)
            join(at, [x, y, (y[0], y[1] + V)], out, f)
            return
        for a, b in SIDES:
            act(R(y[0], y[1] + a, y[1] + b), IX(win, lst("inv", 576 + level * 128 + a // 16, 24)), F.Copy)
        for a, b in SIDES:
            part = R(x[0], x[1] + a, x[1] + b)
            tt(part, IX(win, lst("inv", 512 + level * 128 + a // 16, 24)), part, f)
        join(at, [x, y], out, f)

    bufs = [R("BE", 2 * V + j * 256, 2 * V + (j + 1) * 256) for j in range(5)]
    cp(bufs[4], IX(R("BC"), lst("inv", 7 * 64 + 48, 16)))
    for j in range(4):
        act(bufs[j], IX(R("BC"), lst("inv", j * 64 + 48, 16)), F.Copy)
    for j in range(3):
        tt(bufs[j], IX(R("BC"), lst("inv", (6 - j) * 64 + 48, 16)), bufs[j], A.max)
        if j == 1:
            tt(P(PM + V, PM + W), bufs[4], bufs[0], A.max)
    join(PM + V, [("BE", 2 * V + j * 256) for j in (1, 3, 2)], "A1", A.max, 2 * G, V)
    x2 = exchange(3, 1, ("A1", V), ("ld", 8))
    kept = uses(YO, V, 0, [("BA", j * V) for j in range(4)] + [("BE", j * V) for j in range(2)], PM)
    sweep(99)
    zero(ZERO[2], x2)

    home(1, 0, PM, kept, ("BA", 0), "A1", A.max)
    pack(PKS[2], 3584)

    def votes(m, k):
        a = m * KV + k * V
        mm(P(PV[m] + 3 - k, PV[m] + 192, 4), [(R("E", 15 - i, 143 - i), R("VB", a + i, a + V, 16)) for i in range(16)])

    PV = (0, KV)
    for k in range(4):
        act(piece("VB", k, KV), piece("BC", k, 64), F.Sign, bias=col("sm", 12))
    act(R("A3"), R("topb"), F.Copy, scale=BIG)
    if XB:
        mm(P(XC, KV), [(R("ID"), R("A1", 256, V))], False, True)
        act(R("VB", XC, KV), P(XC, KV), F.Sign, bias=col("sm", 11))
    for q in (0, 2, 1, 3):
        act(piece("BE", q), R("A3"), F.Copy, scale=col("fwf", 4 + q))
    for k in range(4):
        b = min((k + 1) * V, XC)
        tt(R("VB", k * V, b), P(k * V, b), R("A1", 0, b - k * V), A.is_le)
        votes(0, k)
    pack(PKS[3], 3584)

    TB = KV - 1728

    def choose(m, early):
        pv, pi = PV[m], 576 * m
        live = P(pv + 192, pv + 384)
        if m == 0:
            dead, later = R("BB", TB + 1536, TB + 1728), P(512, 704)
            tt(live, P(pv, pv + 192), R("CC", 384, 576), A.is_ge)
            tt(dead, P(pv, pv + 192), R("CC", 0, 192), A.is_lt)
        else:
            dead, later = R("tm", 0, 192), P(pv, pv + 192)

        def unpack(a, b):
            ts(R("fui", pi + a, pi + b), R("BB", TB + 387 + 4 * a, TB + 384 + 4 * b, 4), -1.0, A.add)

        def child(s, a, b):
            x = R("fui", 192 + s * 192 + a, 192 + s * 192 + b)
            if s == 0:
                ts(x, R("fui", pi + a, pi + b), 12, A.arith_shift_right, 0x13FF, A.bitwise_and)
            else:
                ts(x, R("fui", pi + a, pi + b), 2 ** 24 + W - 1, A.bitwise_and)
            ts(R("fc", m * 384 + s * 192 + a, m * 384 + s * 192 + b), x, float(W), A.min)

        def spare():
            mm(P(pv, pv + 192), [(R("ID"), R("DU")), (R("N8"), R("BB", TB + 387, TB + 1152, 4))])

        def second():
            for h in range(2):
                tt(R("BB", TB + 1152 + h * 192, TB + 1344 + h * 192), later, R("BB", TB + 383 + h * 192, TB + 575 + h * 192), A.mult)
            for h in range(2):
                scan(R("BB", TB + 768 + h * 192, TB + 960 + h * 192), dead, R("BB", TB + 1152 + h * 192, TB + 1344 + h * 192))

        for h in range(2):
            a = (m * 2 + h) * 192
            tt(R("BB", TB + h * 192, TB + (h + 1) * 192), live, R("A2", a, a + 192), A.mult)
        for h in range(2):
            scan(R("BB", TB + 384 + h * 192, TB + 576 + h * 192), dead, R("BB", TB + h * 192, TB + (h + 1) * 192))
        if m == 0:
            tt(later, P(pv, pv + 192), R("CC", 192, 384), A.is_ge)
        if early:
            weave(weave(hold(unpack, 0, 96) + hold(child, 0, 0, 96), hold(second)), [])
            rest = weave([LAT] + hold(unpack, 96, 192) + hold(child, 0, 96, 192) + hold(child, 1, 96, 192),
                         hold(child, 1, 0, 96) + hold(place, m, 0, 96) + hold(place, m, 96, 192))
            spare()
            return rest
        second()
        unpack(0, 192)
        spare()
        left, right = hold(child, 0, 0, 192), hold(child, 1, 0, 192)
        held[-1].extend([left[0], right[0], left[1], right[1]])

    def place(m, a, b):
        pi = R("fui", 576 * m + a, 576 * m + b)
        ts(R("cli", a, b), pi, 12, A.arith_shift_right)
        ts(R("cli", 192 + a, 192 + b), pi, U - 1, A.bitwise_and)

    def strip(m):
        for s in range(2):
            tt(R("cli", 384 + s * 192, 576 + s * 192), R("cli", s * 192, (s + 1) * 192), P(PV[m], PV[m] + 192), A.max)
        for s in range(2):
            cp(R("fz", m * 384 + s * 192, m * 384 + (s + 1) * 192), R("cli", 384 + s * 192, 576 + s * 192))

    for k in range(V1):
        votes(1, k)
    rest = choose(0, True)

    for q in range(4):
        act(piece("BA", q), IX(R("flw"), lst("fc", q * 48)), F.Copy, scale=col("fwf", q))
    for q in range(4):
        tt(piece("BB", q), IX(R("flw"), lst("fc", 192 + q * 48)), piece("BA", q), A.mult)
        if q < PE_SUM:
            pe(W, V, [("ID", "BB", q * V)], q == 0, q == PE_SUM - 1)
    for k in range(V1, 4):
        votes(1, k)
    join(W, [("BB", q * V) for q in range(PE_SUM, 4)], "i1w", A.add)
    rest = weave([LAT], rest + hold(strip, 0))
    cp(R("sa"), IX(R("i1w", 0, V), lst("sndu", 16, 16)))
    x4 = exchange(4, -1, ("sa", 0), ("i1w", V))
    zero(ZERO[3], x4)
    for q in (0, 2, 1, 3)[:BDE]:
        act(piece("BC", q), IX(R("flw"), lst("fc", 192 + q * 48)), F.Copy, scale=col("fwf", q))
    pv = PV[1]
    act(R("tm", 0, 192), P(pv, pv + 192), F.Sign, bias=1.0)
    act(P(pv + 192, pv + 384), R("tm", 0, 192), F.Relu)
    act(P(pv, pv + 192), R("tm", 0, 192), F.Relu)
    act(R("tm", 0, 192), R("tm", 0, 192), F.Relu, scale=-1.0)
    act(P(pv, pv + 192, 4), P(pv, pv + 192, 4), F.Copy, scale=0.0)
    act(R("tm", 0, 192, 4), R("tm", 0, 192, 4), F.Copy, scale=0.0)
    for q in (0, 2, 1, 3)[BDE:]:
        act(piece("BC", q), IX(R("flw"), lst("fc", 192 + q * 48)), F.Copy, scale=col("fwf", q))
    weave(weave(hold(choose, 1, False), rest), [])
    place(1, 0, 192)
    strip(1)

    PO, PA, PG, PB, PY = 0, V, 1536, 2048, 3072
    oP = P(PO, PO + V)

    def target(n, m, s, q):
        return IX(R("WW", n * U, (n + 1) * U + STRIP), lst("fz", m * 384 + s * 192 + q * 48))

    def part(n, m, a, b):
        return IX(R("WW", n * U, (n + 1) * U + STRIP), lst("fz", m * 384 + 336 + a // 16, (b - a) // 16))

    def ghosts(n, first, us=(0, 1, 2, 3), last=False):
        mm(P(PG, PG + 2 * G), [(R("ID"), R("WW", n * U + u * W + V, n * U + (u + 1) * W)) for u in us], first, last)

    def halve(a, b):
        if ONE:
            dma("g", [(R("WW", a, a + W + V), R("WW", b, b + W + V))], accum_op=A.add)
        else:
            dma("g", [(R("WW", a + u * W, a + u * W + V), R("WW", b + u * W, b + u * W + V)) for u in range(2)], accum_op=A.add)

    def done(n, first, last=False, how="raw"):
        if how == "half":
            dma("g", [(R("WW", n * U, n * U + 2 * W), R("WW", n * U + 2 * W, (n + 1) * U))], accum_op=A.add)
            ghosts(n, first, (0, 1), last)
        elif how == "v":
            halve(n * U, n * U + 2 * W)
        elif ONE:
            ghosts(n, first, (0,))
            halve(n * U, n * U + 2 * W)
            ghosts(n, False, (1, 2, 3), last)
        else:
            ghosts(n, first, last=last)
            halve(n * U, n * U + 2 * W)

    def pair(x, y):
        for a, b in SIDES:
            tt(P(PA + a, PA + b), R("WW", x[1] + a, x[1] + b), R("WW", y[1] + a, y[1] + b), A.add)

    def finish(wins, plan, last, fill_in, ahead, out, n, land, scale, res):
        wa, wb, wc, wd = wins
        vpre, pre, post, share, two, how = plan
        halves = [("WW", w * U + u * W) for w in ((wa, wc) if two else (wa, wb, wc)) for u in (0, 1)]
        mine, halves = halves[:vpre], halves[vpre:]
        if two == 1:
            halve(wa * U, wb * U)
        for j in range(pre):
            pe(PB, V, [("ID",) + halves[j]], j == 0, j == pre + post - 1)
        done(wc, False, DG != "p", how)
        if two == 2:
            halve(wa * U, wb * U)
        last()
        if DG == "p":
            ghosts(wd, False, last=True)
        for j in range(pre, pre + post):
            pe(PB, V, [("ID",) + halves[j]], j == 0, j == pre + post - 1)
        fill_in()
        if how == "v":
            join(PG, [("WW", wc * U + u * W + V) for u in range(4)], None, A.add, 2 * G)
        if mine:
            pair(*mine[:2])
            join(PA, mine[2:], None, A.add)
        gs = [R("WW", wd * U + u * W + V, wd * U + (u + 1) * W) for u in range(4)]
        if DG == "v":
            join(PG, [("WW", wd * U + u * W + V) for u in range(4)], None if scale else out, A.add, 2 * G)
        if DG == "w":
            tt(gs[0], gs[0], gs[1], A.add)
            tt(gs[2], gs[2], gs[3], A.add)
            join(PG, [("WW", wd * U + u * W + V) for u in (0, 2)], None if scale else out, A.add, 2 * G)
        if scale or DG == "p":
            act(R(out), P(PG, PG + 2 * G), F.Copy, scale=scale or 1.0)
        exchange(n, 1, (out, 0), ("ld", land * LD + 8))
        ahead()
        todo = [("WW", wd * U + u * W) for u in range(4)] + halves[pre + post:]
        kept = todo.pop()
        if not mine:
            pair(*todo[:2])
            todo = todo[2:]
        if not pre + post:
            join(PA, todo, None, A.add)
            return PA, kept
        join(PA, todo, "A1", A.add)
        join(PB, [("A1", 0)], None, A.add)
        return PB, kept

    oS = R("A3")
    pe(PO, V, [("ID", "A3", 0)])

    def edge(q):
        tt(piece("BB", q), IX(R("i1w"), lst("fc", 576 + q * 48)), piece("BB", q), A.mult)

    for h in (0, 1):
        for q in (h, h + 2):
            act(piece("BB", q), IX(R("i1w"), lst("fc", 384 + q * 48)), F.Copy, scale=col("fwf", 4 + q))
        for q in (h, h + 2):
            tt(piece("BE", q), IX(R("i1w"), lst("fc", 576 + q * 48)), piece("BE", q), A.mult)
        for q in (h, h + 2):
            act(target(4 * h, 1, 0, q), piece("BE", q), F.Silu)
        if h == 0:
            for q in (0, 2):
                tt(target(2, 1, 1, q), oS, piece("BB", q), A.mult)
            done(0, True, how=GH2[0])
            done(2, False, PLAN2[5] == "v", GH2[1])
    tt(target(6, 1, 1, 1), oS, piece("BB", 1), A.mult)
    if CUT2 < V:
        tt(R("BE", CUT2, V), R("BB", 3 * V + CUT2, 4 * V), P(PO + CUT2, PO + V), A.mult)
    if CUT2:
        tt(part(6, 1, 0, CUT2), R("A3", 0, CUT2), R("BB", 3 * V, 3 * V + CUT2), A.mult)
    order = (0, 2, 1, 3)

    def edges(qs):
        for q in qs:
            edge(q)

    def last():
        if CUT2 < V:
            act(part(6, 1, CUT2, V), R("BE", CUT2, V), F.Silu)
        act(oP, piece("BC", 2), F.Copy)

    EARLY = ((0, 256, PB + V), (256, V, PG))

    def ahead():
        for a, b, at in EARLY[::-1]:
            act(P(at, at + b - a), R("BC", a, b), F.Copy)

    at, kept = finish((0, 2, 4, 6), PLAN2, last, lambda: edges(order[:YIN]), ahead, "sa", 5, 1, None, "A1")

    def gather_yi(qs):
        for q in qs:
            if YS == "p":
                pe(PY, V, [("ID", "BB", q * V)], q == order[0], q == order[3])
            elif q != order[0]:
                dma("g", [(piece("BB", order[0]), piece("BB", q))], accum_op=A.add)

    gather_yi(order[:YIN])
    if YS != "p":
        act(P(PY, PY + V), piece("BC", 3), F.Copy)
    home(1, 1, at, kept, ("BE", V), "A1", A.add)
    act(P(PA + CUT1, PA + V), R("BA", 3 * V + CUT1, 4 * V), F.Copy)

    oS = R("A1", 0, V)

    def product(name, q, at, a=0):
        x = R(name, q * V + a, (q + 1) * V)
        if OP == "pre":
            tt(x, P(at + a, at + V), R("A1", a, V), A.mult)
        else:
            tt(x, x, P(PO + a, PO + V), A.mult)

    for a, b, at in EARLY:
        tt(R("BC", a, b), P(at, at + b - a), R("A1", a, b), A.mult)
    pe(PB, V, [("ID", "BC", V)])
    tt(piece("BC", 2), oP, oS, A.mult)
    if YS == "p":
        pe(PO, V, [("ID", "BC", 3 * V) if OP == "pre" else ("ID", "A1", 0)])
    for a, b, at in EARLY:
        act(IX(R("WW", U, 2 * U + STRIP), lst("fz", a // 16, (b - a) // 16)), R("BC", a, b), F.Silu)
    act(target(1, 0, 0, 2), piece("BC", 2), F.Silu)
    done(1, True, how=GH1[0])
    tt(target(3, 0, 1, 0), oS, piece("BA", 0), A.mult)
    if CUT1 < V:
        product("BA", 3, PA, CUT1)
        act(part(7, 0, CUT1, V), R("BA", 3 * V + CUT1, 4 * V), F.Silu)
    product("BC", 1, PB)
    product("BC", 3, PO if YS == "p" else PY)
    act(target(5, 0, 0, 1), piece("BC", 1), F.Silu)
    tt(target(3, 0, 1, 2), oS, piece("BA", 2), A.mult)
    done(3, False, PLAN1[5] == "v", GH1[1])
    tt(target(7, 0, 1, 1), oS, piece("BA", 1), A.mult)
    if CUT1:
        tt(part(7, 0, 0, CUT1), R("A1", 0, CUT1), R("BA", 3 * V, 3 * V + CUT1), A.mult)
    at, kept = finish((1, 3, 7, 5), PLAN1, lambda: act(target(5, 0, 0, 3), piece("BC", 3), F.Silu), lambda: edges(order[YIN:]),
                      lambda: None, "sa", 6, 2, None, None)
    gather_yi(order[YIN:])
    if YS == "p":
        act(R("A2"), P(PY, PY + V), F.Copy)
    dma("y", [(H("yi"), R("A2") if YS == "p" else piece("BB", order[0]))])
    home(0, 2, at, kept, ("BC", 0), None, A.add)
    small = -at % 512 or 512
    lo, hi = (0, small), (small, V)
    for (a, b), q in zip((lo, hi), "sv" if small == 256 else "vs"):
        if q == "s":
            act(R("A3", a, b), P(at + a, at + b), F.Copy, scale=1.0 / BIG)
        else:
            ts(R("A3", a, b), P(at + a, at + b), 1.0 / BIG, A.mult)
    dma("y", [(H("yo"), R("A3"))])

    wait("g", list(count.items()))
